import numpy as np, ml_dtypes
CORES = [23,119,17,113]
N = 4
BF = ml_dtypes.bfloat16
W, R, P, STEPS, HOPS, SHIFT = 2048, 4096, 256, 4, 4, 1
def parts(rng):
    h = rng.integers(0, 256, (N, 8, 16, P)); w = rng.integers(0, 256, (N, 8, 16, 1)); t = rng.integers(700, 1300, (N, 8, 16, 1))
    m = rng.random((N, 8, W)) < rng.choice(np.array([0.1, 0.25, 0.5]), (N, 8, 1))
    return h, w, t, m, rng.integers(0, R, (N, 8, 16, W)), rng.integers(0, 256, (N, 8, 16, R))
def pack(h, w, t, m, o, r):
    m = m.astype(np.int32); m[..., 0] = 1
    b = lambda v, n: np.ascontiguousarray(v.reshape(N, 128, n)).astype(np.float32).astype(BF)
    i = lambda v, n: np.ascontiguousarray(v.reshape(N, 128, n)).astype(np.int32)
    return {"h0": b(h, P), "w": b(w, 1), "th": i(t, 1), "marks": m, "owner": i(o, W), "hdr": b(r, R)}
def far(rng, h, t, o, r, g, u=None):
    r[:, g] = rng.integers(128, 192, (N, 16, R))
    goal = np.where(np.arange(R) % 2 == 0, 4, 0) + rng.integers(0, 4, (N, R))
    r[:, g, 15] = 128 + ((goal - np.sum(r[:, g, :15], axis=1)) & 63)
    o[:, g] = (o[:, g] & -2) + (np.arange(16) & 1)[:, None]
    h[:, g] = rng.integers(0, 16, (N, 16, P))
    if u is not None: h[:, g, 0] = u >> 4; h[:, g, 1] = u & 15
    h[:, g, 15] = (-np.sum(h[:, g, :15], axis=1)) & 63
    t[:, g] = rng.integers(1300, 1751, (N, 16, 1))
def setup_inputs(rng):
    return pack(*parts(rng))
def setup_inputs_crowd(rng):
    h, w, t, m, o, r = parts(rng)
    w[:, 0::4] = 0; t[:, 0::4] = rng.integers(500, 1100, (N, 2, 16, 1))
    w[:, 1::4] = 0; w[:, 1::4, 0] = rng.integers(1, 4, (N, 2, 1)); h[:, 1::4, 0] = rng.integers(0, 3, (N, 2, P))
    w[:, 2::4] = 128 * rng.integers(0, 2, (N, 2, 16, 1))
    n = P // 16; lane = np.arange(P)
    far(rng, h, t, o, r, 4)
    start = rng.integers(0, n, (N, 16)); start[:, 0::4] = 0; start[:, 1::4] = n - 1; start[:, 3::4] = 1
    near = (lane >> 4) < start[:, lane & 15]
    h[:, 4] = np.where(near[:, None, :], rng.integers(128, 192, (N, 16, P)), h[:, 4])
    k = np.arange(256); found = np.unique((((k * k) >> 5) + k) & (W - 16), return_index=True)[1]
    order = np.argsort(rng.random((N, 16, len(found))), axis=-1)[..., :n]
    far(rng, h, t, o, r, 7, found[order].transpose(0, 2, 1).reshape(N, P))
    w[:, 7] = 0; w[:, 7, 0] = 16; w[:, 7, 1] = 1; m[:, 7] = True
    return pack(h, w, t, m, o, r)
def setup_inputs_ends(rng):
    h, w, t, m, o, r = parts(rng)
    k = np.arange(4096); tops = np.flatnonzero(((((k * k) >> 5) + k) & (W - 16)) == W - 16)
    u = rng.integers(0, 4096, (N, 6, P)); u[..., 0::32] = 0; u[..., 15::32] = rng.choice(tops, u[..., 15::32].shape)
    u[:, 4, 5::8] = rng.choice(tops, u[:, 4, 5::8].shape)
    w[:, :6] = 0; w[:, :6, 0] = 16; w[:, :6, 1] = 1; h[:, :6, 0] = u >> 4; h[:, :6, 1] = u & 15
    m[:, 0] = False; m[:, 1] = True; m[:, 2] = False; m[:, 2, W - 1] = True; m[:, 3] = True; m[:, 3, W - 1] = False; m[:, 4] = False; m[:, 4, 1] = True; m[:, 4, W - 16] = True
    t[:, 0:4:2] = rng.integers(0, 900, (N, 2, 16, 1)); t[:, 1] = rng.choice(np.array([0, 4096]), (N, 16, 1)); t[:, 5] = 0; t[:, 6] = 4096
    w[:, 7] = 255 - rng.integers(0, 16, (N, 16, 1)); h[:, 7] = 255 - rng.integers(0, 24, (N, 16, P)); w[0, 7] = 255; h[0, 7, :, 0::32] = 255
    return pack(h, w, t, m, o, r)
def setup_inputs_ties(rng):
    h, w, t, m, o, r = parts(rng)
    unit = rng.choice(np.array([8, 16]), (N, 8, 1, 1)); h = unit * (h // unit); r = unit * (r // unit)
    t = unit * (t // unit) + rng.choice(np.array([0, 0, 0, 1, -1]), t.shape)
    w[:, :2] = 0; m[:, :2, :16] = True; h[:, 1, :, :16] = 0; h[:, 1, 0, 1:16:2] = 1
    i = np.arange(16)
    for q in range(N):
        t[q, 0, :, 0] = np.sum(np.abs(r[q, 0][:, o[q, 0, :, 0]] - h[q, 0, :, 0:1]), axis=0)
        t[q, 1, :, 0] = np.sum(np.abs(r[q, 1][:, o[q, 1, i, i]] - h[q, 1, :, :16]), axis=0) + (i % 2 == 0)
    return pack(h, w, t, m, o, r)
def setup_inputs_alike(rng):
    h, w, t, m, o, r = parts(rng)
    o[:, ::2] = rng.choice(np.array([0, R - 1, R // 2, 3]), (N, 4, 16, W)); o[:, 1::4] = o[:, 1::4, :1].copy()
    r[..., 0] = 0; r[..., R - 1] = 255
    h[..., 0::7] = 0; h[..., 1::7] = 255; h[..., 3::7] = r[..., R // 2][..., None]
    t[:, 2] = 1
    t[:, 4] = 4080; t[:, 4, 1::4] = rng.choice(np.array([4081, 4096]), (N, 4, 1)); o[:, 4, 1::4] = R - 1; o[:, 4, 12] = 3
    t[:, 6] = 0; o[:, 6, 1::4] = R // 2; o[:, 6, 0] = 3
    return pack(h, w, t, m, o, r)
def setup_inputs_spread(rng):
    h, w, t, m, o, r = parts(rng)
    h = (np.exp2(8 * rng.random((N, 8, 1, P))) * rng.random((N, 8, 16, P))).astype(np.int64)
    r = (np.exp2(8 * rng.random((N, 8, 1, R))) * rng.random((N, 8, 16, R))).astype(np.int64)
    w = np.minimum(np.exp2(8 * rng.random((N, 8, 16, 1))).astype(np.int64), 255)
    t = np.minimum(np.exp2(12 * rng.random((N, 8, 16, 1))).astype(np.int64), 4096)
    m = rng.random((N, 8, W)) < np.exp2(-8 * rng.random((N, 8, 1)))
    o = np.minimum((R * rng.random((N, 8, 16, W)) ** 3).astype(np.int64), R - 1)
    return pack(h, w, t, m, o, r)
def check_inputs(d):
    bad = []
    for k, hi in (("h0", 255), ("w", 255), ("th", 4096), ("marks", 1), ("owner", R - 1), ("hdr", 255)):
        v = np.asarray(d[k]).astype(np.float32)
        if not np.all((v >= 0) & (v <= hi) & (v == np.floor(v))): bad.append("range of " + k)
    if not np.all(np.asarray(d["marks"])[..., 0] == 1): bad.append("address 0 is a boundary")
    return bad
def reference(h0, w, th, marks, owner, hdr):
    h = h0.astype(np.float32).astype(np.int64).reshape(N, 8, 16, P); wt = w.astype(np.float32).astype(np.int64).reshape(N, 8, 16, 1)
    t = th.astype(np.int64).reshape(N, 8, 1, 16); m = marks > 0; o = owner.astype(np.int64).reshape(N, 8, 16, W)
    r = hdr.astype(np.float32).astype(np.int32).reshape(N, 8, 16, R)
    port = np.arange(P) & 15; slot = np.arange(16)
    for step in range(STEPS):
        u = np.add.reduce(wt * h, axis=2) & 4095
        x = ((((u * u) >> 5) + u) & (W - 16)) + port
        top = np.maximum.accumulate(np.where(m, np.arange(W), 0), axis=2)
        a = np.take_along_axis(top, x, 2); b = np.take_along_axis(top, (a - 1) & (W - 1), 2)
        ra = np.take_along_axis(o, a[:, :, None, :], 3); rb = np.take_along_axis(o, b[:, :, None, :], 3)
        new = []
        for q in range(N):
            ids = np.ascontiguousarray(ra[q].transpose(0, 2, 1)).reshape(8, 1, P * 16)
            v = np.take_along_axis(r[q], ids, 2).reshape(8, 16, P, 16)
            d = np.add.reduce(np.abs(v - h[q][..., None]), axis=1)
            n = np.where(d < t[q], slot, (d >> 2) & 15)
            e = np.zeros((8, P), np.int64) + port
            for hop in range(HOPS):
                e = np.take_along_axis(n, e[..., None], 2)[..., 0]
            done = np.take_along_axis(n, e[..., None], 2)[..., 0] == e
            ve = np.take_along_axis(v, e[:, None, :, None], 3)[..., 0]
            new.append(np.where(done[:, None, :], (h[q] + ve) >> 1, np.abs(h[q] - ve)))
            col = np.where(slot[None, :, None] == e[:, None, :], rb[q], ra[q])
            for g in range(8):
                lanes = np.flatnonzero(~done[g])
                xs, first = np.unique(x[q, g, lanes], return_index=True)
                o[q, g][:, xs] = col[g][:, lanes[first]]
                m[q, g, xs] = True
        h = np.roll(np.stack(new), SHIFT, axis=0)
    return {"yh": h.reshape(N, 128, P).astype(np.float32).astype(BF), "yo": o.reshape(N, 128, W).astype(np.float32), "ym": m.astype(np.float32)}

@@ -1,0 +1,457 @@
+from concourse.mybir import AluOpType as A, ActivationFunctionType as F
+
+N, STEPS, W, R, P = 4, 4, 2048, 4096, 256
+PIECES = [(12, 16, "v", 64), (8, 12, "a", 32), (4, 8, "v", 64), (0, 4, "v", 32)]
+GROUPS = [(0, 1), (2, 3)]
+NPC = len(PIECES)
+TW = W + P
+HEXP = "vvvgvavgvvvgvavg"
+
+SCRATCH = {
+    "HD": ("sbuf", [128, R], "bfloat16"), "OW": ("sbuf", [128, W], "int32"), "MK": ("sbuf", [128, 128], "int32"),
+    "MB": ("sbuf", [128, 128], "bfloat16"), "WT": ("sbuf", [128, 1], "bfloat16"), "TI": ("sbuf", [128, 1], "int32"),
+    "YO": ("sbuf", [128, W], "float32"), "MZ": ("sbuf", [128, TW], "float32"), "NM": ("sbuf", [128, TW], "float32"),
+    "ZP": ("sbuf", [128, W + 8], "float32"), "YM": ("sbuf", [128, W], "float32"),
+    "CM": ("sbuf", [128, 2048], "bfloat16"), "SR": ("sbuf", [128, 2048], "bfloat16"),
+    "BA": ("sbuf", [2, 128], "bfloat16"), "BR": ("sbuf", [2, 128], "bfloat16"),
+    "CA": ("sbuf", [2, 64], "bfloat16"), "CR": ("sbuf", [2, 64], "bfloat16"),
+    "HX": ("sbuf", [128, 16 * P], "bfloat16"), "AB": ("sbuf", [128, 16 * P], "bfloat16"),
+}
+for _d, _w, _ns in (("float32", 1, "SC SQ TH BIG SB KB"), ("int32", 1, "PI SI SJ"),
+                    ("bfloat16", 128, "ON B1 BO HB ID IH NI S1 S2 DB BW G0"),
+                    ("float32", 16, "IK OH T0 TR XF FR AL AM DW DT XQ DU T2 T3 DM DX"), ("int32", 16, "UI UA UB UP UX OI"),
+                    ("uint16", 16, "LX LA SL EL"), ("bfloat16", 512, "WU HL"), ("float32", 512, "DG"),
+                    ("float32", 64, "IQ MQ RS ZE UM US ZM ZS EM ES FM FS"), ("float32", 128, "JS G1"),
+                    ("float32", P, "ZA ZB DZ NA DE"), ("int32", P, "NX NN FD CL"), ("uint16", P, "LP"),
+                    ("bfloat16", P, "NB Y SG E4 DS TD QD")):
+    for _n in _ns.split():
+        SCRATCH[_n] = ("sbuf", [128, _w], _d)
+for _b in range(8):
+    SCRATCH["ps%d" % _b] = ("psum", [128, 512], "float32")
+for _t in range(STEPS + 1):
+    SCRATCH["hb%d" % _t] = ("sbuf", [128, P], "bfloat16")
+    SCRATCH["hn%d" % _t] = ("sbuf", [128, P], "bfloat16")
+for _p in range(NPC):
+    SCRATCH["D%d" % _p] = ("sbuf", [128, 256 * (PIECES[_p][1] - PIECES[_p][0])], "bfloat16")
+SEMAPHORES = ["qv", "qa", "qp", "qg", "ls"] + ["dm%d" % k for k in range(24)] + ["ar%d" % t for t in range(1, STEPS + 1)]
+
+
+def rank_program(g, core, T, topo):
+    rank = T.rank_of(core)
+    if rank is None:
+        return
+    dst = T.cores[(rank + 1) % N]
+    rid, pid, _e = topo.addr(dst)
+    mask = topo.mask(core, dst)
+    ne = len(topo.engines(core, dst))
+    eng = {"v": g.vector, "a": g.scalar, "p": g.tensor, "g": g, "s": g.sync}
+    CY = 1.0e-3
+    ops, pr = [], [0.0]
+
+    def r(n, lo=0, hi=None, st=1):
+        return (n, lo, SCRATCH[n][1][1] if hi is None else hi, st)
+
+    def ap(x):
+        if not isinstance(x, tuple):
+            return x
+        b, lo, hi, st = x
+        if SCRATCH[b][1][0] == 2:
+            return T[b][0:2, lo:hi]
+        return T[b][:, lo:hi] if st == 1 else T[b][:, lo:hi:st]
+
+    def cnt(x):
+        return -(-(x[2] - x[1]) // x[3])
+
+    def ps(x):
+        return isinstance(x, tuple) and x[0][:2] == "ps"
+
+    def two(*xs):
+        return all(SCRATCH[x[0]][2] in ("bfloat16", "uint16") for x in xs)
+
+    def op(q, fn, rd, wr, dur, sem=None, lat=0.0):
+        ops.append({"q": q, "fn": fn, "rd": [x for x in rd if isinstance(x, tuple)], "wr": wr, "dur": dur,
+                    "sem": sem, "lat": lat, "pr": pr[0]})
+
+    def tt(o, a, b, f):
+        c = cnt(o) * (1 if ps(a) or ps(b) else 2)
+        op("v", lambda e: e.tensor_tensor(out=ap(o), in0=ap(a), in1=ap(b), op=f), [a, b], [o], max(64, c) * CY)
+
+    def ts(o, a, s1, f0, s2=None, f1=None):
+        c = cnt(o) * (0.5 if two(o, a) else 1)
+        if f1 is None:
+            fn = lambda e: e.tensor_scalar(out=ap(o), in0=ap(a), scalar1=ap(s1), scalar2=None, op0=f0)
+        else:
+            fn = lambda e: e.tensor_scalar(out=ap(o), in0=ap(a), scalar1=ap(s1), scalar2=ap(s2), op0=f0, op1=f1)
+        op("v", fn, [a, s1, s2], [o], max(64, c) * CY)
+
+    def cp(o, a):
+        c = cnt(o) * (0.5 if two(o, a) else 1)
+        op("v", lambda e: e.tensor_copy(out=ap(o), in_=ap(a)), [a], [o], max(64, c) * CY)
+
+    def scan(o, a, b, ini=0.0, o0=A.mult, o1=A.add):
+        op("v", lambda e: e.tensor_tensor_scan(out=ap(o), data0=ap(a), data1=ap(b), initial=ap(ini), op0=o0, op1=o1),
+           [a, b, ini], [o], max(64, cnt(o)) * CY)
+
+    def ms(o, k):
+        op("v", lambda e: e.memset(ap(o), k), [], [o], max(64, cnt(o) * (0.5 if two(o) else 1)) * CY)
+
+    def act(o, a, f, bias=0.0, scale=1.0):
+        op("a", lambda e: e.activation(out=ap(o), in_=ap(a), func=f, bias=ap(bias), scale=ap(scale)), [a, bias, scale], [o],
+           max(64, cnt(o)) * CY + 0.03)
+
+    def gat(q, o, w, off, in1=None):
+        d = 0.05 + 1.5 * cnt(o) * CY
+        if q == "a":
+            op("a", lambda e: e.activation(out=ap(o), in_=ap(w).indirect(ap(off)), func=F.Copy), [w, off], [o], d + 0.015)
+        elif in1 is None:
+            op("v", lambda e: e.tensor_scalar(out=ap(o), in0=ap(w).indirect(ap(off)), scalar1=-1.0, scalar2=None, op0=A.mult),
+               [w, off], [o], d)
+        else:
+            op("v", lambda e: e.tensor_tensor(out=ap(o), in0=ap(w).indirect(ap(off)), in1=ap(in1), op=A.subtract),
+               [w, off, in1], [o], d)
+
+    def mm(o, pairs, x4=1):
+        def fn(e):
+            last = None
+            for k, (l, x) in enumerate(pairs):
+                last = e.matmul(ap(o), ap(l), ap(x), k == 0, k == len(pairs) - 1)
+            return last
+        op("p", fn, [y for x in pairs for y in x], [o], len(pairs) * max(64, cnt(o)) * CY * x4)
+
+    ndma = [0]
+
+    def dma(q, o_fn, i_fn, rd, wr, dur):
+        s = "dm%d" % ndma[0]
+        ndma[0] += 1
+        op(q, lambda e: e.dma_start(out=o_fn(), in_=i_fn()), rd, wr, 0.1, sem=(s, 16), lat=dur)
+
+    dma("s", lambda: T.MK[:], lambda: T.marks[:], [], [r("MK")], 2.0)
+    dma("a", lambda: T.hb0[:], lambda: T.h0[:], [], [r("hb0")], 2.0)
+    for b in range(4):
+        lo, hi = 512 * b, 512 * b + 512
+        dma("s", lambda lo=lo, hi=hi: T.OW[:, lo:hi], lambda lo=lo, hi=hi: T.owner[:, lo:hi], [], [r("OW", lo, hi)], 2.5 + b)
+    dma("s", lambda: T.WT[:], lambda: T.w[:], [], [r("WT")], 2.0)
+    dma("s", lambda: T.HD[:], lambda: T.hdr[:], [], [r("HD")], 7.0)
+    dma("s", lambda: T.TI[:], lambda: T.th[:], [], [r("TI")], 3.0)
+
+    def iota(o, pat, base, cm):
+        op("g", lambda e: e.iota(ap(o), pat, base, cm, allow_small_or_imprecise_dtypes=True), [], [o],
+           0.13 + 2 * cnt(o) * CY)
+
+    def sel(o, a, pat, f, base, cm, fill=0.0):
+        op("g", lambda e: e.affine_select(out=ap(o), in_=ap(a), pattern=pat, compare_op=f, fill=fill, base=base,
+                                          channel_multiplier=cm), [a], [o], 0.17 + 2 * cnt(o) * CY)
+    iota(r("PI"), [[0, 1]], 0, 1)
+    ms(r("ON"), 1.0)
+    ts(r("SI"), r("PI"), 15, A.bitwise_and)
+    cp(r("SC"), r("SI"))
+    sel(r("B1"), r("ON"), [[-16, 8], [0, 16]], A.is_ge, 0, 1)
+    sel(r("BO"), r("B1"), [[16, 8], [0, 16]], A.is_ge, 15, -1)
+    iota(r("IK"), [[1, 16]], 0, 0)
+    ts(r("OH"), r("IK"), r("SC"), A.is_equal)
+    for k in range(16):
+        act(r("SR", 128 * k, 128 * k + 128), r("BO"), F.Copy, 0.0, r("OH", k, k + 1))
+    cp(r("MB"), r("MK"))
+    ms(r("ZP", 0, 8), 0.0)
+    for b in range(4):
+        lo, hi = 512 * b, 512 * b + 512
+        for k in range(4 * b, 4 * b + 4):
+            mm(r("ps%d" % b, 128 * (k % 4), 128 * (k % 4) + 128), [(r("SR", 128 * k, 128 * k + 128), r("MB"))])
+        m, n2 = r("ps%d" % b), r("ps%d" % (4 + b))
+        act(n2, m, F.Copy, 8192.0, -8192.0)
+        act(r("NM", lo, hi), m, F.Copy, -1 / 4096, 8192.0)
+        tt(r("MZ", lo, hi), n2, r("OW", lo, hi), A.subtract)
+        scan(r("ZP", 8 + lo, 8 + hi), r("NM", lo, hi), r("MZ", lo, hi), r("ZP", 7 + lo, 8 + lo) if b else 0.0, A.add, A.min)
+    cp(r("ZP", 7, 8), r("ZP", W + 7, W + 8))
+    for n in ("WU", "DG", "HL"):
+        ms(r(n), 0.0)
+    for k in range(4):
+        ms(r("CM", 512 * k, 512 * k + 512), 0.0)
+    ts(r("SJ"), r("SI"), 2, A.arith_shift_right)
+    cp(r("SQ"), r("SJ"))
+    iota(r("IQ"), [[0, 16], [1, 4]], 0, 0)
+    ts(r("MQ"), r("IQ"), r("SQ"), A.is_equal)
+    ts(r("RS"), r("IQ"), 0.0, A.is_gt)
+    ts(r("BW"), r("BO"), r("WT"), A.mult)
+    for s in range(4):
+        cp(r("WU", 128 * s + s, 128 * s + 128, 4), r("BW", s, 128, 4))
+    sel(r("ID"), r("ON"), [[-1, 128]], A.is_equal, 0, 1)
+    act(r("NI"), r("ID"), F.Copy, 0.0, -1.0)
+    for s in range(16):
+        act(r("CM", 128 * s + s, 128 * s + 128, 16), r("BO", 0, 128, 16), F.Copy)
+    cp(r("TH"), r("TI"))
+    ts(r("BIG"), r("SC"), 4.0, A.mult, 4096.0, A.add)
+    ts(r("SB"), r("SC"), -1.0, A.mult, 0.5, A.add)
+    for s in range(4):
+        act(r("DG", 128 * s + s, 128 * s + 128, 4), r("ID", s, 128, 4), F.Copy)
+    sel(r("S1"), r("ON"), [[-1, 128]], A.is_equal, 1, 1)
+    sel(r("S2"), r("ON"), [[-1, 128]], A.is_equal, -15, 1)
+    tt(r("S1"), r("S1"), r("BO"), A.mult)
+    tt(r("S2"), r("S2"), r("BO"), A.mult)
+    tt(r("S2"), r("S2"), r("S1"), A.subtract)
+    tt(r("DB"), r("S2"), r("ID"), A.add)
+    iota(r("JS"), [[0, 8], [1, 16]], 0, 0)
+    ts(r("G1"), r("JS"), r("SC"), A.is_ge, 2.0, A.mult)
+    ts(r("G0"), r("G1"), -1.0, A.add)
+    ts(r("HB"), r("BO"), 0.5, A.mult)
+    for s in range(4):
+        cp(r("HL", 128 * s + s, 128 * s + 128, 4), r("HB", s, 128, 4))
+    iota(r("BA"), [[0, 8], [16, 16]], 0, 0)
+    sel(r("BR"), r("BA"), [[0, 128]], A.is_equal, 0, 1, 1.0)
+    iota(r("CA"), [[0, 4], [256, 4], [0, 4]], 0, 0)
+    sel(r("CR"), r("CA"), [[0, 64]], A.not_equal, 0, 1, 1.0)
+    ts(r("IH"), r("ID"), 0.5, A.mult)
+    iota(r("T0"), [[16, 16]], W, 0)
+    ts(r("TR"), r("T0"), r("SC"), A.add)
+    ms(r("ZE"), 8192.0)
+    ms(r("KB"), 8192.0)
+    for ks in GROUPS:
+        c0 = min(PIECES[k][0] for k in ks)
+        ms(r("DU", c0, c0 + 1), 0.0)
+
+    SZ = r("ZP", 8, 8 + W)
+
+    def front(t):
+        hb, u = "hb%d" % t, r("ps4", 0, 64)
+        mm(u, [(r("WU", 128 * s, 128 * s + 128), r(hb, s, P, 4)) for s in range(4)])
+        tt(r("UM"), u, r("MQ"), A.mult)
+        scan(r("US"), r("RS"), r("UM"))
+        cp(r("UI"), r("US", 3, 64, 4))
+        ts(r("UA"), r("UI"), 4095, A.bitwise_and)
+        ts(r("UB"), r("UA"), 32, A.add)
+        tt(r("UP"), r("UA"), r("UB"), A.mult)
+        ts(r("UX"), r("UP"), 5, A.arith_shift_right, 2032, A.bitwise_and)
+        ts(r("LX"), r("UX"), r("SC"), A.add)
+        ts(r("XF"), r("UX"), r("SC"), A.add)
+        for s in range(16):
+            o, i = r("HX", s, 16 * P, 16), r(hb)
+            if HEXP[s] == "a":
+                act(o, i, F.Copy)
+            elif HEXP[s] == "v":
+                cp(o, i)
+            else:
+                sel(o, i, [[0, P]], A.is_gt, 1, 0)
+        gat("v", r("LP"), SZ, r("LX"))
+
+    def before(t):
+        zw, za = r("ps4", 64, 128), r("ps4", 128, 384)
+        gat("a", r("ZA"), SZ, r("LX"))
+        mm(zw, [(r("DG", 128 * s, 128 * s + 128), r("ZA", s, P, 4)) for s in range(4)], x4=4)
+        tt(r("ZM"), zw, r("MQ"), A.mult)
+        scan(r("ZS"), r("RS"), r("ZM"))
+        cp(r("OI"), r("ZS", 3, 64, 4))
+        tt(r("FR"), r("ZS", 3, 64, 4), r("OI"), A.subtract)
+        ts(r("AL"), r("FR"), 4096.0, A.mult, 7.0, A.add)
+        tt(r("AM"), r("AL"), r("XF"), A.add)
+        cp(r("LA"), r("AM"))
+        gat("a", r("ZB"), r("ZP"), r("LA"))
+        act(za, r("ZA"), F.Copy)
+        tt(r("DZ"), r("ZB"), za, A.subtract)
+
+    def wrap(c0, c1):
+        return [(r("BR"), r("CR", 0, 4 * (c1 - c0)))] + \
+            [(r("HL", 128 * s, 128 * s + 128), r("Y", 16 * c0 + s, 16 * c1, 4)) for s in range(4)]
+
+    def rules(t, p):
+        c0, c1, q, ck = PIECES[p]
+        nl, q4, L0, L1 = 16 * (c1 - c0), 4 * (c1 - c0), 16 * c0, 16 * c1
+        hb, D, bk = "hb%d" % t, "D%d" % p, "ps%d" % p
+        for l in range(0, nl, ck):
+            v = r(D, 16 * l, 16 * (l + ck))
+            lp, hx, ab = r("LP", L0 + l, L0 + l + ck), r("HX", 16 * (L0 + l), 16 * (L0 + l + ck)), \
+                r("AB", 16 * (L0 + l), 16 * (L0 + l + ck))
+            if q == "v":
+                gat("v", v, r("HD"), lp, hx)
+                act(ab, v, F.Abs)
+            else:
+                df = r("ps%d" % (6 + (l // ck) % 2), 0, 16 * ck)
+                gat("a", v, r("HD"), lp)
+                mm(df, [(r("NI"), hx), (r("ID"), v)])
+                act(ab, df, F.Abs)
+        d, w0, ad, dl, eb, dn = [r(bk, 64 * k, 64 * k + nl) for k in range(6)]
+        ew = r(bk, 448, 448 + q4)
+        x = lambda n: r(n, L0, L1)
+        y = lambda n, st=1: r(n, 4 * c0 + st - 1, 4 * c1, st)
+        mm(d, [(r("CM", 128 * s, 128 * s + 128), r("AB", 16 * L0 + s, 16 * L1, 16)) for s in range(16)])
+        ts(x("NA"), d, r("TH"), A.is_lt, r("BIG"), A.mult)
+        tt(x("NX"), x("NA"), d, A.max)
+        ts(x("NN"), x("NX"), 2, A.arith_shift_right, 15, A.bitwise_and)
+        cp(x("NB"), x("NN"))
+        mm(dl, [(r("DB"), x("NB"))])
+        for k in range(5):
+            if k:
+                act(x("SG"), eb, F.Sign, r("SB"))
+            if k == 4:
+                act(x("E4"), eb, F.Copy)
+            tt(x("Y"), x("SG") if k else r("G0", 0, nl), dl, A.mult)
+            mm(eb, [(r("HB"), x("Y"))])
+            if k == 3:
+                mm(ew, wrap(c0, c1))
+                tt(y("EM"), ew, y("MQ"), A.mult)
+                scan(y("ES"), y("RS"), y("EM"))
+                cp(r("EL", c0, c1), y("ES", 4))
+        gat("a", x("DS"), r(D), r("EL", c0, c1))
+        if q == "a":
+            mm(ad, [(r("ID"), x("DS")), (r("NI"), x(hb))])
+        act(ad, ad if q == "a" else x("DS"), F.Abs)
+        mm(w0, [(r("IH"), x("DS")), (r("IH") if q == "a" else r("ID"), x(hb))])
+        ts(x("FD"), w0, -0.25, A.add)
+        tt(x("TD"), x("FD"), ad, A.subtract)
+        tt(dn, x("E4"), eb, A.is_equal)
+        tt(x("QD"), x("TD"), dn, A.mult)
+        tt(x("hn%d" % t), x("QD"), ad, A.add)
+
+    def send(t):
+        nh, hn, arr = "hb%d" % (t + 1), r("hn%d" % t), "ar%d" % (t + 1)
+        op("g", lambda e: e.remote_dma(T[nh][:], ap(hn), T.sem[arr], T.sem.ls, pid, rid, mask),
+           [hn], [r(nh)], 1.5, sem=(arr, ne), lat=2.0)
+
+    def calls(t, ks):
+        c0, c1 = min(PIECES[k][0] for k in ks), max(PIECES[k][1] for k in ks)
+        L0, L1 = 16 * c0, 16 * c1
+        e4p, za = r("ps4", 384, 384 + L1 - L0), r("ps4", 128 + L0, 128 + L1)
+        y = lambda n, st=1: r(n, 4 * c0 + st - 1, 4 * c1, st)
+        x = lambda n, a=0, b=0: r(n, c0 + a, c1 - b)
+        z = lambda n: r(n, L0, L1)
+        fw = r("ps5", 4 * c0, 4 * c1)
+        mm(fw, wrap(c0, c1))
+        tt(y("FM"), fw, y("MQ"), A.mult)
+        scan(y("FS"), y("RS"), y("FM"))
+        tt(x("DW"), y("FS", 4), y("ES", 4), A.is_equal)
+        tt(x("DT"), x("DW"), x("TR"), A.mult)
+        tt(x("XQ"), x("DT"), x("XF"), A.max)
+        tt(x("DU", 1), x("XQ", 1), x("XQ", 0, 1), A.is_equal)
+        tt(x("T2", 2), x("XQ", 2), x("XQ", 0, 2), A.is_equal)
+        tt(x("T3", 3), x("XQ", 3), x("XQ", 0, 3), A.is_equal)
+        tt(x("DU", 2), x("DU", 2), x("T2", 2), A.max)
+        tt(x("DU", 3), x("DU", 3), x("T3", 3), A.max)
+        tt(x("DM"), x("DU"), x("TR"), A.mult)
+        tt(x("DX"), x("DM"), x("XQ"), A.max)
+        cp(x("SL"), x("DX"))
+        ts(e4p, z("E4"), r("SC"), A.is_equal)
+        tt(z("DE"), z("DZ"), e4p, A.mult)
+        tt(z("CL"), z("DE"), za, A.add)
+        for c in range(c1 - 4, c0 - 1, -4):
+            off, col = r("SL", c, c + 4), r("CL", 16 * c, 16 * c + 64)
+            op("v", lambda e, off=off, col=col: e.tensor_copy(out=ap(r("MZ")).indirect(ap(off)), in_=ap(col)),
+               [off, col], [r("MZ")], 0.05 + 64 * 3.0 * CY)
+            op("a", lambda e, off=off: e.activation(out=ap(r("NM")).indirect(ap(off)), in_=ap(r("ZE")), func=F.Silu),
+               [off, r("ZE")], [r("NM")], 0.065 + 64 * 3.0 * CY)
+
+    for t in range(STEPS):
+        front(t)
+        for p in range(NPC):
+            pr[0] = 1.0 * (NPC - 1 - p)
+            rules(t, p)
+        send(t)
+        pr[0] = 0.0
+        before(t)
+        for ks in GROUPS:
+            calls(t, ks)
+        if t < STEPS - 1:
+            scan(SZ, r("NM", 0, W), r("MZ", 0, W), 0.0, A.add, A.min)
+            cp(r("ZP", 7, 8), r("ZP", W + 7, W + 8))
+    for b in range(4):
+        lo, hi, m = 512 * b, 512 * b + 512, r("ps%d" % b)
+        act(m, r("NM", lo, hi), F.Relu, r("KB"), -2.0)
+        tt(r("YO", lo, hi), m, r("MZ", lo, hi), A.subtract)
+        dma("s", lambda lo=lo, hi=hi: T.yo[:, lo:hi], lambda lo=lo, hi=hi: T.YO[:, lo:hi], [r("YO", lo, hi)], [], 5.0)
+        act(r("YM", lo, hi), m, F.Copy, 1.0, -1 / 8192)
+    dma("s", lambda: T.ym[:], lambda: T.YM[0:128:16, :], [r("YM")], [], 2.0)
+    dma("s", lambda: T.yh[:], lambda: T["hb%d" % STEPS][:], [r("hb%d" % STEPS)], [], 2.0)
+
+    emit(g, T, ops, eng, ne)
+
+
+def meet(x, y):
+    if x[1] >= y[2] or y[1] >= x[2]:
+        return False
+    return not (x[3] == y[3] and x[3] > 1 and (x[1] - y[1]) % x[3])
+
+
+def covers(x, y):
+    return x[3] == 1 and x[1] <= y[1] and x[2] >= y[2]
+
+
+def emit(g, T, ops, eng, ne):
+    n = len(ops)
+    dep = [dict() for _ in range(n)]
+    hist = {}
+    for i, o in enumerate(ops):
+        for wr, xs in ((False, o["rd"]), (True, o["wr"])):
+            for x in xs:
+                psum = x[0][:2] == "ps"
+                for (j, y, w) in hist.get(x[0], []):
+                    same = ops[j]["q"] == o["q"] and ops[j]["sem"] is None
+                    if (wr or w) and meet(x, y):
+                        wait = (w or not same) and not (same and o["q"] == "p" and w and wr)
+                        dep[i][j] = dep[i].get(j, False) or wait
+                    elif psum:
+                        dep[i][j] = dep[i].get(j, False) or not same
+        for wr, xs in ((False, o["rd"]), (True, o["wr"])):
+            for x in xs:
+                h = hist.setdefault(x[0], [])
+                if wr:
+                    h[:] = [z for z in h if z[0] == i or not covers(x, z[1])]
+                h.append((i, x, wr))
+    succ = [[] for _ in range(n)]
+    for i in range(n):
+        for j in dep[i]:
+            succ[j].append(i)
+    HOP = 0.1
+    tail = [0.0] * n
+    for i in range(n - 1, -1, -1):
+        o = ops[i]
+        tail[i] = o["dur"] + o["lat"] + max([tail[k] + HOP for k in succ[i]], default=0.0)
+    left = [len(dep[i]) for i in range(n)]
+    avail = [0.0] * n
+    ready = {q: [] for q in eng}
+    for i in range(n):
+        if not left[i]:
+            ready[ops[i]["q"]].append(i)
+    free = {q: 0.0 for q in eng}
+    order = []
+    while len(order) < n:
+        t0, q = min((max(free[q], min(avail[i] for i in ready[q])), q) for q in eng if ready[q])
+        i = max((k for k in ready[q] if avail[k] <= t0 + 1e-9), key=lambda k: (tail[k] + ops[k]["pr"], -k))
+        ready[q].remove(i)
+        o = ops[i]
+        free[q] = t0 + o["dur"]
+        for k in succ[i]:
+            avail[k] = max(avail[k], t0 + o["dur"] + o["lat"] + HOP if dep[k][i] else t0)
+            left[k] -= 1
+            if not left[k]:
+                ready[ops[k]["q"]].append(k)
+        order.append(i)
+    count = {q: 0 for q in eng}
+    mark, know, after, place = {}, {q: {} for q in eng}, {}, {}
+    final = {}
+    for i in order:
+        o = ops[i]
+        q = o["q"]
+        kn = know[q]
+        for j in sorted((j for j in dep[i] if dep[i][j]), key=lambda j: -place[j]):
+            s, v = mark[j]
+            if kn.get(s, 0) >= v:
+                continue
+            eng[q].wait_ge(T.sem[s], v)
+            for s2, v2 in after[j].items():
+                if kn.get(s2, 0) < v2:
+                    kn[s2] = v2
+        ins = o["fn"](eng[q])
+        remote = o["sem"] is not None and o["sem"][0][:2] == "ar"
+        if o["sem"] is None:
+            count[q] += 1
+            mark[i] = ("q" + q, count[q])
+            ins.then_inc(T.sem["q" + q], 1)
+        else:
+            mark[i] = o["sem"]
+            if not remote:
+                ins.then_inc(T.sem[o["sem"][0]], 16)
+        final[mark[i][0]] = mark[i][1]
+        after[i] = {} if remote else dict(kn)
+        after[i][mark[i][0]] = mark[i][1]
+        place[i] = len(place)
+    for s, v in final.items():
+        g.wait_ge(T.sem[s], v)
+    g.wait_ge(T.sem.ls, ne * STEPS)

@@ -1,29 +1,32 @@
 from concourse.mybir import AluOpType as A, ActivationFunctionType as F
 
 N, STEPS, W, R, P = 4, 4, 2048, 4096, 256
-PIECES = [(12, 16, "v", 64), (8, 12, "a", 32), (4, 8, "v", 64), (0, 4, "v", 32)]
-GROUPS = [(0, 1), (2, 3)]
+PIECES = [(12, 16, (("a", 32), ("v", 32))), (8, 12, (("v", 64),)), (4, 8, (("a", 32), ("v", 32))), (0, 4, (("v", 32), ("v", 32)))]
+PARTS = [(0, 1), (2, 3)]
+HEXP = ["agaagaagaagaagav", "vgvavgvvvgvavgvv"]
+OPEN = True
 NPC = len(PIECES)
-TW = W + P
-HEXP = "vvvgvavgvvvgvavg"
+TW = W + 16
+BIG = float(2 ** 21)
+MAGIC = 1.5 * 2 ** 23
+HOP = 0.12
+PRI = [3.0, 2.0, 1.0, 0.0]
+PEC = 1.0
 
 SCRATCH = {
     "HD": ("sbuf", [128, R], "bfloat16"), "OW": ("sbuf", [128, W], "int32"), "MK": ("sbuf", [128, 128], "int32"),
-    "MB": ("sbuf", [128, 128], "bfloat16"), "WT": ("sbuf", [128, 1], "bfloat16"), "TI": ("sbuf", [128, 1], "int32"),
-    "YO": ("sbuf", [128, W], "float32"), "MZ": ("sbuf", [128, TW], "float32"), "NM": ("sbuf", [128, TW], "float32"),
+    "WT": ("sbuf", [128, 1], "bfloat16"), "TI": ("sbuf", [128, 1], "int32"),
+    "YO": ("sbuf", [128, TW], "float32"), "MZ": ("sbuf", [128, TW], "float32"), "NM": ("sbuf", [128, TW], "float32"),
     "ZP": ("sbuf", [128, W + 8], "float32"), "YM": ("sbuf", [128, W], "float32"),
     "CM": ("sbuf", [128, 2048], "bfloat16"), "SR": ("sbuf", [128, 2048], "bfloat16"),
-    "BA": ("sbuf", [2, 128], "bfloat16"), "BR": ("sbuf", [2, 128], "bfloat16"),
-    "CA": ("sbuf", [2, 64], "bfloat16"), "CR": ("sbuf", [2, 64], "bfloat16"),
-    "HX": ("sbuf", [128, 16 * P], "bfloat16"), "AB": ("sbuf", [128, 16 * P], "bfloat16"),
 }
-for _d, _w, _ns in (("float32", 1, "SC SQ TH BIG SB KB"), ("int32", 1, "PI SI SJ"),
-                    ("bfloat16", 128, "ON B1 BO HB ID IH NI S1 S2 DB BW G0"),
-                    ("float32", 16, "IK OH T0 TR XF FR AL AM DW DT XQ DU T2 T3 DM DX"), ("int32", 16, "UI UA UB UP UX OI"),
-                    ("uint16", 16, "LX LA SL EL"), ("bfloat16", 512, "WU HL"), ("float32", 512, "DG"),
-                    ("float32", 64, "IQ MQ RS ZE UM US ZM ZS EM ES FM FS"), ("float32", 128, "JS G1"),
-                    ("float32", P, "ZA ZB DZ NA DE"), ("int32", P, "NX NN FD CL"), ("uint16", P, "LP"),
-                    ("bfloat16", P, "NB Y SG E4 DS TD QD")):
+for _d, _w, _ns in (("float32", 1, "SC SQ TB NB SX TR QB"), ("int32", 1, "PI SI SJ"),
+                    ("bfloat16", 128, "ON B1 BO ID IH NI S1 DD BW MB OH0 I16 I128 I72 Ba Bb Bc Bd Be Bf Bg Bh"),
+                    ("float32", 16, "IK OH XF ZR FR AM ZE ZF"), ("int32", 16, "UI UA UB UP UX"),
+                    ("uint16", 16, "LX LA EL"), ("uint16", 32, "SL"), ("bfloat16", 512, "WU HE HN"), ("float32", 512, "DG"),
+                    ("float32", 64, "IQ RU RZ US ZS RT"), ("bfloat16", 64, "MQ VQ VN"), ("float32", 128, "JS RX ES"),
+                    ("float32", P, "ZA ZM ZI DE NA"), ("int32", P, "DZ A1 NX NN"), ("uint16", P, "LP"),
+                    ("bfloat16", P, "NP C0 C1 C2 C3 G DN DS AD"), ("bfloat16", 16 * P, "HX AB D")):
     for _n in _ns.split():
         SCRATCH[_n] = ("sbuf", [128, _w], _d)
 for _b in range(8):
@@ -31,9 +34,8 @@ for _b in range(8):
 for _t in range(STEPS + 1):
     SCRATCH["hb%d" % _t] = ("sbuf", [128, P], "bfloat16")
     SCRATCH["hn%d" % _t] = ("sbuf", [128, P], "bfloat16")
-for _p in range(NPC):
-    SCRATCH["D%d" % _p] = ("sbuf", [128, 256 * (PIECES[_p][1] - PIECES[_p][0])], "bfloat16")
-SEMAPHORES = ["qv", "qa", "qp", "qg", "ls"] + ["dm%d" % k for k in range(24)] + ["ar%d" % t for t in range(1, STEPS + 1)]
+SEMAPHORES = ["qv", "qa", "qp", "qg", "ls"] + ["dm%d" % k for k in range(24)] + \
+    ["ar%d_%d" % (t, h) for t in range(1, STEPS + 1) for h in range(4)]
 
 
 def rank_program(g, core, T, topo):
@@ -88,16 +90,16 @@ def rank_program(g, core, T, topo):
         c = cnt(o) * (0.5 if two(o, a) else 1)
         op("v", lambda e: e.tensor_copy(out=ap(o), in_=ap(a)), [a], [o], max(64, c) * CY)
 
-    def scan(o, a, b, ini=0.0, o0=A.mult, o1=A.add):
+    def scan(o, a, b, ini, o0, o1):
         op("v", lambda e: e.tensor_tensor_scan(out=ap(o), data0=ap(a), data1=ap(b), initial=ap(ini), op0=o0, op1=o1),
            [a, b, ini], [o], max(64, cnt(o)) * CY)
 
     def ms(o, k):
         op("v", lambda e: e.memset(ap(o), k), [], [o], max(64, cnt(o) * (0.5 if two(o) else 1)) * CY)
 
-    def act(o, a, f, bias=0.0, scale=1.0):
+    def act(o, a, f, bias=0.0, scale=1.0, more=0.0):
         op("a", lambda e: e.activation(out=ap(o), in_=ap(a), func=f, bias=ap(bias), scale=ap(scale)), [a, bias, scale], [o],
-           max(64, cnt(o)) * CY + 0.03)
+           max(64, cnt(o)) * CY + more)
 
     def gat(q, o, w, off, in1=None):
         d = 0.05 + 1.5 * cnt(o) * CY
@@ -110,29 +112,20 @@ def rank_program(g, core, T, topo):
             op("v", lambda e: e.tensor_tensor(out=ap(o), in0=ap(w).indirect(ap(off)), in1=ap(in1), op=A.subtract),
                [w, off, in1], [o], d)
 
-    def mm(o, pairs, x4=1):
-        def fn(e):
-            last = None
-            for k, (l, x) in enumerate(pairs):
-                last = e.matmul(ap(o), ap(l), ap(x), k == 0, k == len(pairs) - 1)
-            return last
-        op("p", fn, [y for x in pairs for y in x], [o], len(pairs) * max(64, cnt(o)) * CY * x4)
+    def mm(o, l, x, start, stop):
+        op("p", lambda e: e.matmul(ap(o), ap(l), ap(x), start, stop), [l, x], [o],
+           max(64, cnt(o)) * CY * PEC * (4 if SCRATCH[x[0]][2] == "float32" else 1))
+
+    def mms(o, pairs, start=True, stop=True):
+        for k, (l, x) in enumerate(pairs):
+            mm(o, l, x, start and k == 0, (stop or not OPEN) and k == len(pairs) - 1)
 
     ndma = [0]
 
     def dma(q, o_fn, i_fn, rd, wr, dur):
         s = "dm%d" % ndma[0]
         ndma[0] += 1
-        op(q, lambda e: e.dma_start(out=o_fn(), in_=i_fn()), rd, wr, 0.1, sem=(s, 16), lat=dur)
-
-    dma("s", lambda: T.MK[:], lambda: T.marks[:], [], [r("MK")], 2.0)
-    dma("a", lambda: T.hb0[:], lambda: T.h0[:], [], [r("hb0")], 2.0)
-    for b in range(4):
-        lo, hi = 512 * b, 512 * b + 512
-        dma("s", lambda lo=lo, hi=hi: T.OW[:, lo:hi], lambda lo=lo, hi=hi: T.owner[:, lo:hi], [], [r("OW", lo, hi)], 2.5 + b)
-    dma("s", lambda: T.WT[:], lambda: T.w[:], [], [r("WT")], 2.0)
-    dma("s", lambda: T.HD[:], lambda: T.hdr[:], [], [r("HD")], 7.0)
-    dma("s", lambda: T.TI[:], lambda: T.th[:], [], [r("TI")], 3.0)
+        op(q, lambda e: e.dma_start(out=o_fn(), in_=i_fn()), rd, wr, 0.06, sem=(s, 16), lat=dur)
 
     def iota(o, pat, base, cm):
         op("g", lambda e: e.iota(ap(o), pat, base, cm, allow_small_or_imprecise_dtypes=True), [], [o],
@@ -141,6 +134,17 @@ def rank_program(g, core, T, topo):
     def sel(o, a, pat, f, base, cm, fill=0.0):
         op("g", lambda e: e.affine_select(out=ap(o), in_=ap(a), pattern=pat, compare_op=f, fill=fill, base=base,
                                           channel_multiplier=cm), [a], [o], 0.17 + 2 * cnt(o) * CY)
+
+    loads = [("s", "MK", "marks", None, 2.0), ("a", "hb0", "h0", None, 2.2), ("a", "WT", "w", None, 2.2)] + \
+        [("s", "OW", "owner", 512 * b, 3.0 + b) for b in range(4)] + [("s", "HD", "hdr", None, 10.0), ("a", "TI", "th", None, 2.2)]
+    for k, (q, b, src, lo, dur) in enumerate(loads):
+        pr[0] = 1000.0 - 20 * k
+        if lo is None:
+            dma(q, lambda b=b: T[b][:], lambda src=src: T[src][:], [], [r(b)], dur)
+        else:
+            dma(q, lambda lo=lo: T.OW[:, lo:lo + 512], lambda lo=lo: T.owner[:, lo:lo + 512], [], [r("OW", lo, lo + 512)], dur)
+    pr[0] = 0.0
+
     iota(r("PI"), [[0, 1]], 0, 1)
     ms(r("ON"), 1.0)
     ts(r("SI"), r("PI"), 15, A.bitwise_and)
@@ -150,217 +154,212 @@ def rank_program(g, core, T, topo):
     iota(r("IK"), [[1, 16]], 0, 0)
     ts(r("OH"), r("IK"), r("SC"), A.is_equal)
     for k in range(16):
-        act(r("SR", 128 * k, 128 * k + 128), r("BO"), F.Copy, 0.0, r("OH", k, k + 1))
-    cp(r("MB"), r("MK"))
+        if k % 2:
+            act(r("SR", 128 * k, 128 * k + 128), r("BO"), F.Copy, 0.0, r("OH", k, k + 1))
+        else:
+            ts(r("SR", 128 * k, 128 * k + 128), r("BO"), r("OH", k, k + 1), A.mult)
+    ts(r("MB"), r("MK"), -2.0, A.mult, 1.0, A.add)
     ms(r("ZP", 0, 8), 0.0)
     for b in range(4):
         lo, hi = 512 * b, 512 * b + 512
         for k in range(4 * b, 4 * b + 4):
-            mm(r("ps%d" % b, 128 * (k % 4), 128 * (k % 4) + 128), [(r("SR", 128 * k, 128 * k + 128), r("MB"))])
-        m, n2 = r("ps%d" % b), r("ps%d" % (4 + b))
-        act(n2, m, F.Copy, 8192.0, -8192.0)
-        act(r("NM", lo, hi), m, F.Copy, -1 / 4096, 8192.0)
-        tt(r("MZ", lo, hi), n2, r("OW", lo, hi), A.subtract)
+            mm(r("ps%d" % b, 128 * (k % 4), 128 * (k % 4) + 128), r("SR", 128 * k, 128 * k + 128), r("MB"), True, True)
+        m = r("ps%d" % b)
+        act(r("NM", lo, hi), m, F.Copy, 2048.0, -2048.0 - 1 / 4096)
+        tt(r("MZ", lo, hi), m, r("OW", lo, hi), A.mult)
         scan(r("ZP", 8 + lo, 8 + hi), r("NM", lo, hi), r("MZ", lo, hi), r("ZP", 7 + lo, 8 + lo) if b else 0.0, A.add, A.min)
-    cp(r("ZP", 7, 8), r("ZP", W + 7, W + 8))
-    for n in ("WU", "DG", "HL"):
+    act(r("ZP", 7, 8), r("ZP", W + 7, W + 8), F.Copy)
+    for n in ("WU", "DG", "HE", "HN", "RU", "RZ", "RX"):
         ms(r(n), 0.0)
     for k in range(4):
         ms(r("CM", 512 * k, 512 * k + 512), 0.0)
     ts(r("SJ"), r("SI"), 2, A.arith_shift_right)
     cp(r("SQ"), r("SJ"))
     iota(r("IQ"), [[0, 16], [1, 4]], 0, 0)
-    ts(r("MQ"), r("IQ"), r("SQ"), A.is_equal)
-    ts(r("RS"), r("IQ"), 0.0, A.is_gt)
+    ts(r("VQ"), r("IQ"), r("SQ"), A.is_equal, BIG, A.mult)
+    ts(r("VN"), r("VQ"), -BIG, A.add)
+    ms(r("RU", 3, 64, 4), -BIG)
+    ms(r("RZ", 0, 64, 4), -4 * BIG)
     ts(r("BW"), r("BO"), r("WT"), A.mult)
+    sel(r("ID"), r("ON"), [[-1, 128]], A.is_equal, 0, 1)
     for s in range(4):
         cp(r("WU", 128 * s + s, 128 * s + 128, 4), r("BW", s, 128, 4))
-    sel(r("ID"), r("ON"), [[-1, 128]], A.is_equal, 0, 1)
-    act(r("NI"), r("ID"), F.Copy, 0.0, -1.0)
+        act(r("DG", 128 * s + s, 128 * s + 128, 4), r("ID", s, 128, 4), F.Copy)
+        act(r("HE", 128 * s + s, 128 * s + 128, 4), r("BO", s, 128, 4), F.Copy, 0.0, -1.0)
+        act(r("HN", 128 * s + s, 128 * s + 128, 4), r("BO", s, 128, 4), F.Copy, 0.0, 8192.0)
     for s in range(16):
         act(r("CM", 128 * s + s, 128 * s + 128, 16), r("BO", 0, 128, 16), F.Copy)
-    cp(r("TH"), r("TI"))
-    ts(r("BIG"), r("SC"), 4.0, A.mult, 4096.0, A.add)
-    ts(r("SB"), r("SC"), -1.0, A.mult, 0.5, A.add)
-    for s in range(4):
-        act(r("DG", 128 * s + s, 128 * s + 128, 4), r("ID", s, 128, 4), F.Copy)
+    for n, src, k in (("NI", "ID", -1.0), ("IH", "ID", 0.5), ("Ba", "BO", 16.0), ("Bb", "BO", -256.0), ("Bc", "BO", 4096.0),
+                      ("Bd", "BO", -65536.0), ("Be", "BO", 512.0), ("Bf", "BO", -512.0)):
+        ts(r(n), r(src), k, A.mult)
+    ts(r("NB"), r("SC"), 4.0, A.mult, -4096.0, A.add)
+    ts(r("TB"), r("TI"), 8192.0, A.mult, r("NB"), A.add)
+    ts(r("NB"), r("SC"), -16.0, A.mult)
+    ts(r("SX"), r("SC"), -BIG, A.add)
+    ts(r("TR"), r("SC"), float(W), A.add)
     sel(r("S1"), r("ON"), [[-1, 128]], A.is_equal, 1, 1)
-    sel(r("S2"), r("ON"), [[-1, 128]], A.is_equal, -15, 1)
     tt(r("S1"), r("S1"), r("BO"), A.mult)
-    tt(r("S2"), r("S2"), r("BO"), A.mult)
-    tt(r("S2"), r("S2"), r("S1"), A.subtract)
-    tt(r("DB"), r("S2"), r("ID"), A.add)
+    tt(r("DD"), r("ID"), r("S1"), A.subtract)
     iota(r("JS"), [[0, 8], [1, 16]], 0, 0)
-    ts(r("G1"), r("JS"), r("SC"), A.is_ge, 2.0, A.mult)
-    ts(r("G0"), r("G1"), -1.0, A.add)
-    ts(r("HB"), r("BO"), 0.5, A.mult)
-    for s in range(4):
-        cp(r("HL", 128 * s + s, 128 * s + 128, 4), r("HB", s, 128, 4))
-    iota(r("BA"), [[0, 8], [16, 16]], 0, 0)
-    sel(r("BR"), r("BA"), [[0, 128]], A.is_equal, 0, 1, 1.0)
-    iota(r("CA"), [[0, 4], [256, 4], [0, 4]], 0, 0)
-    sel(r("CR"), r("CA"), [[0, 64]], A.not_equal, 0, 1, 1.0)
-    ts(r("IH"), r("ID"), 0.5, A.mult)
-    iota(r("T0"), [[16, 16]], W, 0)
-    ts(r("TR"), r("T0"), r("SC"), A.add)
-    ms(r("ZE"), 8192.0)
-    ms(r("KB"), 8192.0)
-    for ks in GROUPS:
-        c0 = min(PIECES[k][0] for k in ks)
-        ms(r("DU", c0, c0 + 1), 0.0)
+    ts(r("OH0"), r("JS"), r("SC"), A.is_equal)
+    ms(r("ZF"), 8192.0)
+    act(r("ZE"), r("ZF"), F.Silu, more=1.3)
+    ms(r("QB"), 1 / 4096)
+    at = {}
+    for part in PARTS:
+        cs = sorted(part, key=lambda p: PIECES[p][0])
+        lo = 8 * PIECES[cs[0]][0]
+        for k, p in enumerate(cs):
+            n4 = 4 * (PIECES[p][1] - PIECES[p][0])
+            at[p] = (lo, lo, lo + n4) if k == 0 else (lo, lo + n4, lo)
+            lo += 2 * n4
+    iota(r("RT", 0, 16), [[256, 16]], 16, 0)
+    ts(r("RT", 16, 17), r("SC"), 16.0, A.mult, -BIG, A.add)
+    for p, (c0, c1, _c) in enumerate(PIECES):
+        ts(r("RX", at[p][1] + 3, at[p][1] + 4 * (c1 - c0), 4), r("RT", 0, c1 - c0), r("RT", 16, 17), A.add)
 
     SZ = r("ZP", 8, 8 + W)
 
-    def front(t):
-        hb, u = "hb%d" % t, r("ps4", 0, 64)
-        mm(u, [(r("WU", 128 * s, 128 * s + 128), r(hb, s, P, 4)) for s in range(4)])
-        tt(r("UM"), u, r("MQ"), A.mult)
-        scan(r("US"), r("RS"), r("UM"))
-        cp(r("UI"), r("US", 3, 64, 4))
-        ts(r("UA"), r("UI"), 4095, A.bitwise_and)
-        ts(r("UB"), r("UA"), 32, A.add)
-        tt(r("UP"), r("UA"), r("UB"), A.mult)
-        ts(r("UX"), r("UP"), 5, A.arith_shift_right, 2032, A.bitwise_and)
-        ts(r("LX"), r("UX"), r("SC"), A.add)
-        ts(r("XF"), r("UX"), r("SC"), A.add)
+    def span(part):
+        return min(PIECES[p][0] for p in part), max(PIECES[p][1] for p in part)
+
+    def front(t, h):
+        c0, c1 = span(PARTS[h])
+        L0, L1, n4 = 16 * c0, 16 * c1, 4 * (c1 - c0)
+        hb, u = "hb%d" % t, r("ps%d" % (2 * PARTS[h][0]), 448, 448 + n4)
+        x = lambda n: r(n, c0, c1)
+        mms(u, [(r("ID"), r("VQ", 0, n4))] + [(r("WU", 128 * s, 128 * s + 128), r(hb, L0 + s, L1, 4)) for s in range(4)])
+        scan(r("US", 4 * c0, 4 * c1), u, r("RU", 0, n4), 0.0, A.max, A.add)
+        cp(x("UI"), r("US", 4 * c0 + 3, 4 * c1, 4))
+        ts(x("UA"), x("UI"), 4095, A.bitwise_and)
+        ts(x("UB"), x("UA"), 32, A.add)
+        tt(x("UP"), x("UA"), x("UB"), A.mult)
+        ts(x("UX"), x("UP"), 5, A.arith_shift_right, 2032, A.bitwise_and)
+        ts(x("LX"), x("UX"), r("SC"), A.add)
+        lo = min(at[p][2] for p in PARTS[h])
+        ts(r("RX", lo + 3, lo + n4, 4), x("UX"), r("SX"), A.add)
         for s in range(16):
-            o, i = r("HX", s, 16 * P, 16), r(hb)
-            if HEXP[s] == "a":
+            o, i = r("HX", 16 * L0 + s, 16 * L1, 16), r(hb, L0, L1)
+            if HEXP[h][s] == "a":
                 act(o, i, F.Copy)
-            elif HEXP[s] == "v":
+            elif HEXP[h][s] == "v":
                 cp(o, i)
             else:
-                sel(o, i, [[0, P]], A.is_gt, 1, 0)
-        gat("v", r("LP"), SZ, r("LX"))
+                sel(o, i, [[0, L1 - L0]], A.is_gt, 1, 0)
+        gat("v", r("LP", L0, L1), SZ, x("LX"))
 
     def before(t):
-        zw, za = r("ps4", 64, 128), r("ps4", 128, 384)
+        zw = r("ps%d" % (2 * NPC - 2), 384, 448)
+        sg = -1.0 if t == STEPS - 1 else 1.0
         gat("a", r("ZA"), SZ, r("LX"))
-        mm(zw, [(r("DG", 128 * s, 128 * s + 128), r("ZA", s, P, 4)) for s in range(4)], x4=4)
-        tt(r("ZM"), zw, r("MQ"), A.mult)
-        scan(r("ZS"), r("RS"), r("ZM"))
-        cp(r("OI"), r("ZS", 3, 64, 4))
-        tt(r("FR"), r("ZS", 3, 64, 4), r("OI"), A.subtract)
-        ts(r("AL"), r("FR"), 4096.0, A.mult, 7.0, A.add)
-        tt(r("AM"), r("AL"), r("XF"), A.add)
-        cp(r("LA"), r("AM"))
-        gat("a", r("ZB"), r("ZP"), r("LA"))
-        act(za, r("ZA"), F.Copy)
-        tt(r("DZ"), r("ZB"), za, A.subtract)
-
-    def wrap(c0, c1):
-        return [(r("BR"), r("CR", 0, 4 * (c1 - c0)))] + \
-            [(r("HL", 128 * s, 128 * s + 128), r("Y", 16 * c0 + s, 16 * c1, 4)) for s in range(4)]
+        mms(zw, [(r("ID"), r("VN"))] + [(r("DG", 128 * s, 128 * s + 128), r("ZA", s, P, 4)) for s in range(4)])
+        scan(r("ZS"), r("RZ"), zw, 0.0, A.add, A.max)
+        ts(r("ZR"), r("ZS", 3, 64, 4), MAGIC, A.add, MAGIC, A.subtract)
+        tt(r("FR"), r("ZS", 3, 64, 4), r("ZR"), A.subtract)
+        ts(r("XF"), r("LX"), 7.0, A.add, 1 / 4096, A.mult)
+        tt(r("AM"), r("FR"), r("XF"), A.add)
+        ts(r("LA"), r("AM"), 4096.0, A.mult)
+        act(r("ZM"), r("ZA"), F.Copy, MAGIC)
+        act(r("ZI"), r("ZM"), F.Copy, -MAGIC)
+        gat("v", r("DZ"), r("ZP"), r("LA"), r("ZI"))
+        if sg < 0:
+            act(r("ZA"), r("ZM"), F.Copy, MAGIC, -1.0)
 
     def rules(t, p):
-        c0, c1, q, ck = PIECES[p]
-        nl, q4, L0, L1 = 16 * (c1 - c0), 4 * (c1 - c0), 16 * c0, 16 * c1
-        hb, D, bk = "hb%d" % t, "D%d" % p, "ps%d" % p
-        for l in range(0, nl, ck):
-            v = r(D, 16 * l, 16 * (l + ck))
-            lp, hx, ab = r("LP", L0 + l, L0 + l + ck), r("HX", 16 * (L0 + l), 16 * (L0 + l + ck)), \
-                r("AB", 16 * (L0 + l), 16 * (L0 + l + ck))
+        c0, c1, chunks = PIECES[p]
+        nl, n4, L0, L1 = 16 * (c1 - c0), 4 * (c1 - c0), 16 * c0, 16 * c1
+        hb, X, Y = "hb%d" % t, "ps%d" % (2 * p), "ps%d" % (2 * p + 1)
+        last = t == STEPS - 1
+        x = lambda n: r(n, L0, L1)
+        l = L0
+        for q, ck in chunks:
+            v, lp, hx, ab = r("D", 16 * l, 16 * (l + ck)), r("LP", l, l + ck), r("HX", 16 * l, 16 * (l + ck)), r("AB", 16 * l, 16 * (l + ck))
             if q == "v":
                 gat("v", v, r("HD"), lp, hx)
                 act(ab, v, F.Abs)
             else:
-                df = r("ps%d" % (6 + (l // ck) % 2), 0, 16 * ck)
+                df = r(Y, 0, 16 * ck)
                 gat("a", v, r("HD"), lp)
-                mm(df, [(r("NI"), hx), (r("ID"), v)])
+                mms(df, [(r("NI"), hx), (r("ID"), v)])
                 act(ab, df, F.Abs)
-        d, w0, ad, dl, eb, dn = [r(bk, 64 * k, 64 * k + nl) for k in range(6)]
-        ew = r(bk, 448, 448 + q4)
-        x = lambda n: r(n, L0, L1)
-        y = lambda n, st=1: r(n, 4 * c0 + st - 1, 4 * c1, st)
-        mm(d, [(r("CM", 128 * s, 128 * s + 128), r("AB", 16 * L0 + s, 16 * L1, 16)) for s in range(16)])
-        ts(x("NA"), d, r("TH"), A.is_lt, r("BIG"), A.mult)
-        tt(x("NX"), x("NA"), d, A.max)
+            l += ck
+        d, y1, a2 = r(X, 0, nl), r(X, 128, 128 + nl), r(X, 0, nl)
+        y0, oh, w0 = r(Y, 0, nl), r(Y, 128, 128 + nl), r(Y, 256, 256 + nl)
+        k = lambda n: r(n, 0, nl)
+        mms(d, [(r("CM", 128 * s, 128 * s + 128), r("AB", 16 * L0 + s, 16 * L1, 16)) for s in range(16)])
+        act(x("NA"), d, F.Identity, r("TB"), -8192.0)
+        tt(x("NX"), d, x("NA"), A.max)
         ts(x("NN"), x("NX"), 2, A.arith_shift_right, 15, A.bitwise_and)
-        cp(x("NB"), x("NN"))
-        mm(dl, [(r("DB"), x("NB"))])
-        for k in range(5):
-            if k:
-                act(x("SG"), eb, F.Sign, r("SB"))
-            if k == 4:
-                act(x("E4"), eb, F.Copy)
-            tt(x("Y"), x("SG") if k else r("G0", 0, nl), dl, A.mult)
-            mm(eb, [(r("HB"), x("Y"))])
-            if k == 3:
-                mm(ew, wrap(c0, c1))
-                tt(y("EM"), ew, y("MQ"), A.mult)
-                scan(y("ES"), y("RS"), y("EM"))
-                cp(r("EL", c0, c1), y("ES", 4))
-        gat("a", x("DS"), r(D), r("EL", c0, c1))
-        if q == "a":
-            mm(ad, [(r("ID"), x("DS")), (r("NI"), x(hb))])
-        act(ad, ad if q == "a" else x("DS"), F.Abs)
-        mm(w0, [(r("IH"), x("DS")), (r("IH") if q == "a" else r("ID"), x(hb))])
-        ts(x("FD"), w0, -0.25, A.add)
-        tt(x("TD"), x("FD"), ad, A.subtract)
-        tt(dn, x("E4"), eb, A.is_equal)
-        tt(x("QD"), x("TD"), dn, A.mult)
-        tt(x("hn%d" % t), x("QD"), ad, A.add)
-
-    def send(t):
-        nh, hn, arr = "hb%d" % (t + 1), r("hn%d" % t), "ar%d" % (t + 1)
-        op("g", lambda e: e.remote_dma(T[nh][:], ap(hn), T.sem[arr], T.sem.ls, pid, rid, mask),
-           [hn], [r(nh)], 1.5, sem=(arr, ne), lat=2.0)
-
-    def calls(t, ks):
-        c0, c1 = min(PIECES[k][0] for k in ks), max(PIECES[k][1] for k in ks)
-        L0, L1 = 16 * c0, 16 * c1
-        e4p, za = r("ps4", 384, 384 + L1 - L0), r("ps4", 128 + L0, 128 + L1)
-        y = lambda n, st=1: r(n, 4 * c0 + st - 1, 4 * c1, st)
-        x = lambda n, a=0, b=0: r(n, c0 + a, c1 - b)
-        z = lambda n: r(n, L0, L1)
-        fw = r("ps5", 4 * c0, 4 * c1)
-        mm(fw, wrap(c0, c1))
-        tt(y("FM"), fw, y("MQ"), A.mult)
-        scan(y("FS"), y("RS"), y("FM"))
-        tt(x("DW"), y("FS", 4), y("ES", 4), A.is_equal)
-        tt(x("DT"), x("DW"), x("TR"), A.mult)
-        tt(x("XQ"), x("DT"), x("XF"), A.max)
-        tt(x("DU", 1), x("XQ", 1), x("XQ", 0, 1), A.is_equal)
-        tt(x("T2", 2), x("XQ", 2), x("XQ", 0, 2), A.is_equal)
-        tt(x("T3", 3), x("XQ", 3), x("XQ", 0, 3), A.is_equal)
-        tt(x("DU", 2), x("DU", 2), x("T2", 2), A.max)
-        tt(x("DU", 3), x("DU", 3), x("T3", 3), A.max)
-        tt(x("DM"), x("DU"), x("TR"), A.mult)
-        tt(x("DX"), x("DM"), x("XQ"), A.max)
-        cp(x("SL"), x("DX"))
-        ts(e4p, z("E4"), r("SC"), A.is_equal)
-        tt(z("DE"), z("DZ"), e4p, A.mult)
-        tt(z("CL"), z("DE"), za, A.add)
-        for c in range(c1 - 4, c0 - 1, -4):
-            off, col = r("SL", c, c + 4), r("CL", 16 * c, 16 * c + 64)
-            op("v", lambda e, off=off, col=col: e.tensor_copy(out=ap(r("MZ")).indirect(ap(off)), in_=ap(col)),
-               [off, col], [r("MZ")], 0.05 + 64 * 3.0 * CY)
+        ts(x("NP"), x("NN"), r("NB"), A.add)
+        tt(x("C0"), x("NN"), k("OH0"), A.mult)
+        for j in range(1, 5):
+            y = y1 if j % 2 else y0
+            mms(y, [(r("ID"), x("NP"))] + [(r("B" + "abcd"[j - 1 - i]), x("C%d" % i)) for i in range(j)])
+            if j < 4:
+                ts(x("C%d" % j), y, 0.0, A.max, 16.0, A.min)
+        s0, se, sx = at[p]
+        wr = lambda a: r(X, 256 + a - s0, 256 + a - s0 + n4)
+        mm(r(X, 256, 256 + 2 * n4), r("ID"), r("VQ", 0, 2 * n4), True, False)
+        ts(x("DN"), y0, r("SC"), A.is_equal)
+        ts(x("G"), y0, 16.0, A.is_lt)
+        for s in range(4):
+            mm(wr(sx), r("HN", 128 * s, 128 * s + 128), r("DN", L0 + s, L1, 4), False, False)
+        mms(oh, [(r("DD"), x("G"))])
+        for s in range(4):
+            mm(wr(se), r("HE", 128 * s, 128 * s + 128), r("G", L0 + s, L1, 4), False, s == 3)
+        tt(x("DE"), oh, x("DZ"), A.mult)
+        scan(r("ES", s0, s0 + 2 * n4), r(X, 256, 256 + 2 * n4), r("RX", s0, s0 + 2 * n4), 0.0, A.max, A.add)
+        ts(r("SL", 2 * c0, 2 * c1, 2), r("ES", sx + 3, sx + n4, 4), r("TR"), A.min)
+        cp(r("EL", c0, c1), r("ES", se + 3, se + n4, 4))
+        tab, base, f = (r("YO"), "ZA", A.subtract) if last else (r("MZ"), "ZI", A.add)
+        for c in range(c1 - 1, c0 - 1, -1):
+            off, de, zi = r("SL", 2 * c, 2 * c + 1), r("DE", 16 * c, 16 * c + 16), r(base, 16 * c, 16 * c + 16)
+            op("v", lambda e, off=off, de=de, zi=zi: e.tensor_tensor(out=ap(tab).indirect(ap(off)), in0=ap(zi), in1=ap(de), op=f),
+               [off, de, zi], [tab], 0.05 + 16 * 3.5 * CY)
             op("a", lambda e, off=off: e.activation(out=ap(r("NM")).indirect(ap(off)), in_=ap(r("ZE")), func=F.Silu),
-               [off, r("ZE")], [r("NM")], 0.065 + 64 * 3.0 * CY)
+               [off, r("ZE")], [r("NM")], 0.065 + 16 * 3.5 * CY)
+        gat("a", x("DS"), r("D", 16 * L0, 16 * L1), r("EL", c0, c1))
+        gat("a", x("AD"), r("AB", 16 * L0, 16 * L1), r("EL", c0, c1))
+        mm(w0, r("Be"), x("DN"), True, False)
+        l = L0
+        for q, ck in chunks:
+            mm(r(Y, 256 + l - L0, 256 + l - L0 + ck), r("IH") if q == "a" else r("ID"), r(hb, l, l + ck), False, False)
+            l += ck
+        mm(a2, r("Bf"), x("DN"), True, False)
+        mm(w0, r("IH"), x("DS"), False, True)
+        mm(a2, r("ID"), x("AD"), False, True)
+        ts(x("A1"), w0, -512.25, A.add)
+        tt(x("hn%d" % t), a2, x("A1"), A.max)
+
+    def send(t, h):
+        c0, c1 = span(PARTS[h])
+        nh, hn, arr = r("hb%d" % (t + 1), 16 * c0, 16 * c1), r("hn%d" % t, 16 * c0, 16 * c1), "ar%d_%d" % (t + 1, h)
+        op("g", lambda e: e.remote_dma(ap(nh), ap(hn), T.sem[arr], T.sem.ls, pid, rid, mask),
+           [hn], [nh], 1.0, sem=(arr, ne), lat=2.0)
 
     for t in range(STEPS):
-        front(t)
-        for p in range(NPC):
-            pr[0] = 1.0 * (NPC - 1 - p)
-            rules(t, p)
-        send(t)
-        pr[0] = 0.0
+        for h in range(len(PARTS)):
+            front(t, h)
         before(t)
-        for ks in GROUPS:
-            calls(t, ks)
+        for h, part in enumerate(PARTS):
+            for p in part:
+                pr[0] = PRI[p]
+                rules(t, p)
+            send(t, h)
+            pr[0] = 0.0
         if t < STEPS - 1:
             scan(SZ, r("NM", 0, W), r("MZ", 0, W), 0.0, A.add, A.min)
-            cp(r("ZP", 7, 8), r("ZP", W + 7, W + 8))
-    for b in range(4):
-        lo, hi, m = 512 * b, 512 * b + 512, r("ps%d" % b)
-        act(m, r("NM", lo, hi), F.Relu, r("KB"), -2.0)
-        tt(r("YO", lo, hi), m, r("MZ", lo, hi), A.subtract)
-        dma("s", lambda lo=lo, hi=hi: T.yo[:, lo:hi], lambda lo=lo, hi=hi: T.YO[:, lo:hi], [r("YO", lo, hi)], [], 5.0)
-        act(r("YM", lo, hi), m, F.Copy, 1.0, -1 / 8192)
+            act(r("ZP", 7, 8), r("ZP", W + 7, W + 8), F.Copy)
+        if t == STEPS - 2:
+            for lo in range(0, W, 512):
+                act(r("YO", lo, lo + 512), r("MZ", lo, lo + 512), F.Abs)
+    dma("s", lambda: T.yo[:], lambda: T.YO[:, 0:W], [r("YO")], [], 5.0)
+    ts(r("YM", 0, W // 2), r("NM", 0, W // 2), 0.0, A.is_gt)
+    act(r("YM", W // 2, W), r("NM", W // 2, W), F.Sign, r("QB"))
     dma("s", lambda: T.ym[:], lambda: T.YM[0:128:16, :], [r("YM")], [], 2.0)
     dma("s", lambda: T.yh[:], lambda: T["hb%d" % STEPS][:], [r("hb%d" % STEPS)], [], 2.0)
 
-    emit(g, T, ops, eng, ne)
+    emit(g, T, ops, eng, ne * STEPS * len(PARTS))
 
 
 def meet(x, y):
@@ -373,7 +372,7 @@ def covers(x, y):
     return x[3] == 1 and x[1] <= y[1] and x[2] >= y[2]
 
 
-def emit(g, T, ops, eng, ne):
+def emit(g, T, ops, eng, sent):
     n = len(ops)
     dep = [dict() for _ in range(n)]
     hist = {}
@@ -393,16 +392,17 @@ def emit(g, T, ops, eng, ne):
                 h = hist.setdefault(x[0], [])
                 if wr:
                     h[:] = [z for z in h if z[0] == i or not covers(x, z[1])]
+                if x[0][:2] == "ps":
+                    h[:] = [z for z in h if ops[z[0]]["q"] != o["q"] or (z[2] and o["q"] != "p")]
                 h.append((i, x, wr))
     succ = [[] for _ in range(n)]
     for i in range(n):
         for j in dep[i]:
             succ[j].append(i)
-    HOP = 0.1
     tail = [0.0] * n
     for i in range(n - 1, -1, -1):
         o = ops[i]
-        tail[i] = o["dur"] + o["lat"] + max([tail[k] + HOP for k in succ[i]], default=0.0)
+        tail[i] = o["dur"] + max([tail[k] + (o["lat"] + HOP if dep[k][i] else 0.0) for k in succ[i]], default=o["lat"])
     left = [len(dep[i]) for i in range(n)]
     avail = [0.0] * n
     ready = {q: [] for q in eng}
@@ -454,4 +454,4 @@ def emit(g, T, ops, eng, ne):
         place[i] = len(place)
     for s, v in final.items():
         g.wait_ge(T.sem[s], v)
-    g.wait_ge(T.sem.ls, ne * STEPS)
+    g.wait_ge(T.sem.ls, sent)

@@ -1,3 +1,4 @@
+import math
 from concourse.mybir import AluOpType as A, ActivationFunctionType as F
 
 N, STEPS, W, R, P = 4, 4, 2048, 4096, 256
@@ -9,9 +10,11 @@ NPC = len(PIECES)
 TW = W + 16
 BIG = float(2 ** 21)
 MAGIC = 1.5 * 2 ** 23
-HOP = 0.12
-PRI = [3.0, 2.0, 1.0, 0.0]
-PEC = 1.0
+HOP = 0.2
+PRI = [0.0, 0.0, 0.0, 0.0]
+PEC = 0.7
+WAW = True
+ABS = 1
 
 SCRATCH = {
     "HD": ("sbuf", [128, R], "bfloat16"), "OW": ("sbuf", [128, W], "int32"), "MK": ("sbuf", [128, 128], "int32"),
@@ -276,7 +279,9 @@ def rank_program(g, core, T, topo):
             v, lp, hx, ab = r("D", 16 * l, 16 * (l + ck)), r("LP", l, l + ck), r("HX", 16 * l, 16 * (l + ck)), r("AB", 16 * l, 16 * (l + ck))
             if q == "v":
                 gat("v", v, r("HD"), lp, hx)
-                act(ab, v, F.Abs)
+                na = ABS if p == NPC - 1 and l + ck == L1 else 1
+                for j in range(na):
+                    act(r("AB", ab[1] + j, ab[2], na), r("D", ab[1] + j, ab[2], na), F.Abs)
             else:
                 df = r(Y, 0, 16 * ck)
                 gat("a", v, r("HD"), lp)
@@ -286,7 +291,8 @@ def rank_program(g, core, T, topo):
         d, y1, a2 = r(X, 0, nl), r(X, 128, 128 + nl), r(X, 0, nl)
         y0, oh, w0 = r(Y, 0, nl), r(Y, 128, 128 + nl), r(Y, 256, 256 + nl)
         k = lambda n: r(n, 0, nl)
-        mms(d, [(r("CM", 128 * s, 128 * s + 128), r("AB", 16 * L0 + s, 16 * L1, 16)) for s in range(16)])
+        mms(d, [(r("CM", 128 * s, 128 * s + 128), r("AB", 16 * L0 + s, 16 * L1, 16))
+                for s in sorted(range(16), key=lambda s: s % ABS)])
         act(x("NA"), d, F.Identity, r("TB"), -8192.0)
         tt(x("NX"), d, x("NA"), A.max)
         ts(x("NN"), x("NX"), 2, A.arith_shift_right, 15, A.bitwise_and)
@@ -365,7 +371,7 @@ def rank_program(g, core, T, topo):
 def meet(x, y):
     if x[1] >= y[2] or y[1] >= x[2]:
         return False
-    return not (x[3] == y[3] and x[3] > 1 and (x[1] - y[1]) % x[3])
+    return (x[1] - y[1]) % math.gcd(x[3], y[3]) == 0
 
 
 def covers(x, y):
@@ -383,7 +389,7 @@ def emit(g, T, ops, eng, sent):
                 for (j, y, w) in hist.get(x[0], []):
                     same = ops[j]["q"] == o["q"] and ops[j]["sem"] is None
                     if (wr or w) and meet(x, y):
-                        wait = (w or not same) and not (same and o["q"] == "p" and w and wr)
+                        wait = not same or (w and not wr) or (w and WAW and o["q"] != "p")
                         dep[i][j] = dep[i].get(j, False) or wait
                     elif psum:
                         dep[i][j] = dep[i].get(j, False) or not same

@@ -2,17 +2,26 @@ import math
 from concourse.mybir import AluOpType as A, ActivationFunctionType as F
 
 N, STEPS, W, R, P = 4, 4, 2048, 4096, 256
-PIECES = [(12, 16, (("a", 32), ("v", 32))), (8, 12, (("v", 64),)), (4, 8, (("a", 32), ("v", 32))), (0, 4, (("v", 32), ("v", 32)))]
+PIECES = [(12, 16, (("v", 32), ("a", 32))), (8, 12, (("v", 32), ("v", 32))), (4, 8, (("v", 32), ("a", 32))), (0, 4, (("v", 32), ("v", 32)))]
 PARTS = [(0, 1), (2, 3)]
-HEXP = ["agaagaagaagaagav", "vgvavgvvvgvavgvv"]
+HEXP = ["agaagaagaagaagag", "agvaggavvgavagva"]
 OPEN = True
 NPC = len(PIECES)
-TW = W + 16
+TW = W + 64
+DED = [4, 4, 4, 2]
+BEFORE = [(0, 1), (2, 3)]
+BPR = [0.0, 0.0, 0.0, 0.0]
 BIG = float(2 ** 21)
 MAGIC = 1.5 * 2 ** 23
 HOP = 0.2
+ROUNDS = 6
+LOG = []
+PERT = {}
 PRI = [0.0, 0.0, 0.0, 0.0]
-PEC = 0.7
+GPR = [0.0, 0.0, 0.0, 0.0]
+FPR = [0.0, 0.0, 0.0, 0.0]
+PEC = 0.5
+CY = 0.83e-3
 WAW = True
 ABS = 1
 
@@ -25,11 +34,13 @@ SCRATCH = {
 }
 for _d, _w, _ns in (("float32", 1, "SC SQ TB NB SX TR QB"), ("int32", 1, "PI SI SJ"),
                     ("bfloat16", 128, "ON B1 BO ID IH NI S1 DD BW MB OH0 I16 I128 I72 Ba Bb Bc Bd Be Bf Bg Bh"),
-                    ("float32", 16, "IK OH XF ZR FR AM ZE ZF"), ("int32", 16, "UI UA UB UP UX"),
+                    ("float32", 16, "IK OH"), ("float32", 64, "ZE ZF"), ("float32", 80, "DA DB DO"),
+                    ("int32", 16, "UI UA UB UP UX ZR FR AM"),
                     ("uint16", 16, "LX LA EL"), ("uint16", 32, "SL"), ("bfloat16", 512, "WU HE HN"), ("float32", 512, "DG"),
-                    ("float32", 64, "IQ RU RZ US ZS RT"), ("bfloat16", 64, "MQ VQ VN"), ("float32", 128, "JS RX ES"),
+                    ("float32", 64, "IQ RU RZ ZS RT"), ("int32", 64, "US UQ UR"), ("bfloat16", 64, "MQ VQ VN"), ("float32", 128, "JS RX ES"),
                     ("float32", P, "ZA ZM ZI DE NA"), ("int32", P, "DZ A1 NX NN"), ("uint16", P, "LP"),
-                    ("bfloat16", P, "NP C0 C1 C2 C3 G DN DS AD"), ("bfloat16", 16 * P, "HX AB D")):
+                    ("bfloat16", P, "NP C0 C1 C2 C3 G DN DS AD"), ("bfloat16", 16 * P, "HX"), ("bfloat16", 32 * P, "D"),
+                    ("bfloat16", 512, "Z5 H32 H64 H96 H128"), ("float32", 1, "KB")):
     for _n in _ns.split():
         SCRATCH[_n] = ("sbuf", [128, _w], _d)
 for _b in range(8):
@@ -50,8 +61,7 @@ def rank_program(g, core, T, topo):
     mask = topo.mask(core, dst)
     ne = len(topo.engines(core, dst))
     eng = {"v": g.vector, "a": g.scalar, "p": g.tensor, "g": g, "s": g.sync}
-    CY = 1.0e-3
-    ops, pr = [], [0.0]
+    ops, pr, tag = [], [0.0], ["c"]
 
     def r(n, lo=0, hi=None, st=1):
         return (n, lo, SCRATCH[n][1][1] if hi is None else hi, st)
@@ -75,7 +85,8 @@ def rank_program(g, core, T, topo):
 
     def op(q, fn, rd, wr, dur, sem=None, lat=0.0):
         ops.append({"q": q, "fn": fn, "rd": [x for x in rd if isinstance(x, tuple)], "wr": wr, "dur": dur,
-                    "sem": sem, "lat": lat, "pr": pr[0]})
+                    "sem": sem, "lat": lat, "pr": pr[0] + PERT.get((q, wr[0][0][:3] if wr else "", tag[0]), 0.0),
+                    "key": (q, wr[0][0][:3] if wr else "", tag[0])})
 
     def tt(o, a, b, f):
         c = cnt(o) * (1 if ps(a) or ps(b) else 2)
@@ -138,8 +149,8 @@ def rank_program(g, core, T, topo):
         op("g", lambda e: e.affine_select(out=ap(o), in_=ap(a), pattern=pat, compare_op=f, fill=fill, base=base,
                                           channel_multiplier=cm), [a], [o], 0.17 + 2 * cnt(o) * CY)
 
-    loads = [("s", "MK", "marks", None, 2.0), ("a", "hb0", "h0", None, 2.2), ("a", "WT", "w", None, 2.2)] + \
-        [("s", "OW", "owner", 512 * b, 3.0 + b) for b in range(4)] + [("s", "HD", "hdr", None, 10.0), ("a", "TI", "th", None, 2.2)]
+    loads = [("s", "MK", "marks", None, 2.5), ("a", "hb0", "h0", None, 2.3), ("a", "WT", "w", None, 2.5)] + \
+        [("s", "OW", "owner", 512 * b, 3.5 + b) for b in range(4)] + [("s", "HD", "hdr", None, 10.6), ("a", "TI", "th", None, 3.5)]
     for k, (q, b, src, lo, dur) in enumerate(loads):
         pr[0] = 1000.0 - 20 * k
         if lo is None:
@@ -191,9 +202,9 @@ def rank_program(g, core, T, topo):
         act(r("HE", 128 * s + s, 128 * s + 128, 4), r("BO", s, 128, 4), F.Copy, 0.0, -1.0)
         act(r("HN", 128 * s + s, 128 * s + 128, 4), r("BO", s, 128, 4), F.Copy, 0.0, 8192.0)
     for s in range(16):
-        act(r("CM", 128 * s + s, 128 * s + 128, 16), r("BO", 0, 128, 16), F.Copy)
+        act(r("CM", 128 * s + s, 128 * s + 128, 16), r("BO", 0, 128, 16), F.Copy, 0.0, 0.5)
     for n, src, k in (("NI", "ID", -1.0), ("IH", "ID", 0.5), ("Ba", "BO", 16.0), ("Bb", "BO", -256.0), ("Bc", "BO", 4096.0),
-                      ("Bd", "BO", -65536.0), ("Be", "BO", 512.0), ("Bf", "BO", -512.0)):
+                      ("Bd", "BO", -65536.0), ("Be", "BO", 512.0), ("Bf", "ID", 2.0), ("Bg", "ID", -0.25), ("Bh", "ID", 0.0)):
         ts(r(n), r(src), k, A.mult)
     ts(r("NB"), r("SC"), 4.0, A.mult, -4096.0, A.add)
     ts(r("TB"), r("TI"), 8192.0, A.mult, r("NB"), A.add)
@@ -209,7 +220,13 @@ def rank_program(g, core, T, topo):
     act(r("ZE"), r("ZF"), F.Silu, more=1.3)
     ms(r("QB"), 1 / 4096)
     at = {}
-    for part in PARTS:
+    pairs = [part[k:k + 2] for part in PARTS for k in range(0, len(part), 2)]
+    ms(r("DA"), 0.0)
+    ms(r("DB"), 4.0)
+    ms(r("DB", 0, 80, 5), 0.0)
+    iota(r("RT", 32, 48), [[0, 4], [16, 4]], W, 0)
+    ts(r("DB", 4, 80, 5), r("RT", 32, 48), r("SC"), A.add, 1 / 8192, A.mult)
+    for part in pairs:
         cs = sorted(part, key=lambda p: PIECES[p][0])
         lo = 8 * PIECES[cs[0]][0]
         for k, p in enumerate(cs):
@@ -219,7 +236,14 @@ def rank_program(g, core, T, topo):
     iota(r("RT", 0, 16), [[256, 16]], 16, 0)
     ts(r("RT", 16, 17), r("SC"), 16.0, A.mult, -BIG, A.add)
     for p, (c0, c1, _c) in enumerate(PIECES):
-        ts(r("RX", at[p][1] + 3, at[p][1] + 4 * (c1 - c0), 4), r("RT", 0, c1 - c0), r("RT", 16, 17), A.add)
+        ts(r("RX", at[p][1] + 3, at[p][1] + 4 * (c1 - c0), 4), r("RT", 0, c1 - c0), r("RT", 16, 17), A.add, 256.0 * (c1 - c0), A.add)
+    for nl in sorted(set(16 * (c1 - c0) for c0, c1, _c in PIECES)):
+        ms(r("H%d" % nl), 0.0)
+        for s in range(4):
+            act(r("H%d" % nl, 128 * s + s, 128 * s + 128, 4), r("BO", s, 128, 4), F.Copy, 0.0, -16.0 * nl)
+    iota(r("UQ"), [[0, 16], [2, 4]], 0, 0)
+    ms(r("KB"), -512.0)
+    ms(r("Z5"), 0.0)
 
     SZ = r("ZP", 8, 8 + W)
 
@@ -233,40 +257,48 @@ def rank_program(g, core, T, topo):
         x = lambda n: r(n, c0, c1)
         mms(u, [(r("ID"), r("VQ", 0, n4))] + [(r("WU", 128 * s, 128 * s + 128), r(hb, L0 + s, L1, 4)) for s in range(4)])
         scan(r("US", 4 * c0, 4 * c1), u, r("RU", 0, n4), 0.0, A.max, A.add)
-        cp(x("UI"), r("US", 4 * c0 + 3, 4 * c1, 4))
-        ts(x("UA"), x("UI"), 4095, A.bitwise_and)
-        ts(x("UB"), x("UA"), 32, A.add)
-        tt(x("UP"), x("UA"), x("UB"), A.mult)
-        ts(x("UX"), x("UP"), 5, A.arith_shift_right, 2032, A.bitwise_and)
+        ts(r("UQ", 4 * c0 + 3, 4 * c1, 4), r("US", 4 * c0 + 3, 4 * c1, 4), 4095, A.bitwise_and)
+        scan(r("UR", 4 * c0, 4 * c1), r("UQ", 4 * c0, 4 * c1), r("UQ", 4 * c0, 4 * c1), 0.0, A.add, A.mult)
+        ts(x("UX"), r("UR", 4 * c0 + 3, 4 * c1, 4), 5, A.arith_shift_right, 2032, A.bitwise_and)
         ts(x("LX"), x("UX"), r("SC"), A.add)
-        lo = min(at[p][2] for p in PARTS[h])
-        ts(r("RX", lo + 3, lo + n4, 4), x("UX"), r("SX"), A.add)
-        for s in range(16):
-            o, i = r("HX", 16 * L0 + s, 16 * L1, 16), r(hb, L0, L1)
+        for pair in pairs:
+            if pair[0] in PARTS[h]:
+                a0, a1 = span(pair)
+                lo = min(at[p][2] for p in pair)
+                ts(r("RX", lo + 3, lo + 4 * (a1 - a0), 4), r("UX", a0, a1), r("SX"), A.add)
+        vs = []
+        for p in PARTS[h]:
+            l = 16 * PIECES[p][0]
+            for q, ck in PIECES[p][2]:
+                vs += [l, l + ck] if q == "v" else []
+                l += ck
+        for s in range(16 if vs else 0):
+            o, i = r("HX", 16 * min(vs) + s, 16 * max(vs), 16), r(hb, min(vs), max(vs))
             if HEXP[h][s] == "a":
                 act(o, i, F.Copy)
             elif HEXP[h][s] == "v":
                 cp(o, i)
             else:
-                sel(o, i, [[0, L1 - L0]], A.is_gt, 1, 0)
+                sel(o, i, [[0, cnt(i)]], A.is_gt, 1, 0)
         gat("v", r("LP", L0, L1), SZ, x("LX"))
 
-    def before(t):
-        zw = r("ps%d" % (2 * NPC - 2), 384, 448)
-        sg = -1.0 if t == STEPS - 1 else 1.0
-        gat("a", r("ZA"), SZ, r("LX"))
-        mms(zw, [(r("ID"), r("VN"))] + [(r("DG", 128 * s, 128 * s + 128), r("ZA", s, P, 4)) for s in range(4)])
-        scan(r("ZS"), r("RZ"), zw, 0.0, A.add, A.max)
-        ts(r("ZR"), r("ZS", 3, 64, 4), MAGIC, A.add, MAGIC, A.subtract)
-        tt(r("FR"), r("ZS", 3, 64, 4), r("ZR"), A.subtract)
-        ts(r("XF"), r("LX"), 7.0, A.add, 1 / 4096, A.mult)
-        tt(r("AM"), r("FR"), r("XF"), A.add)
-        ts(r("LA"), r("AM"), 4096.0, A.mult)
-        act(r("ZM"), r("ZA"), F.Copy, MAGIC)
-        act(r("ZI"), r("ZM"), F.Copy, -MAGIC)
-        gat("v", r("DZ"), r("ZP"), r("LA"), r("ZI"))
-        if sg < 0:
-            act(r("ZA"), r("ZM"), F.Copy, MAGIC, -1.0)
+    def before(t, part):
+        c0, c1 = span(part)
+        n4 = 4 * (c1 - c0)
+        zw = r("ps%d" % (2 * part[-1]), 384, 384 + n4)
+        x, y = lambda n: r(n, c0, c1), lambda n: r(n, 16 * c0, 16 * c1)
+        gat("a", y("ZA"), SZ, x("LX"))
+        mms(zw, [(r("ID"), r("VN", 0, n4))] + [(r("DG", 128 * s, 128 * s + 128), r("ZA", 16 * c0 + s, 16 * c1, 4)) for s in range(4)])
+        scan(r("ZS", 4 * c0, 4 * c1), r("RZ", 0, n4), zw, 0.0, A.add, A.max)
+        ts(x("ZR"), r("ZS", 4 * c0 + 3, 4 * c1, 4), -4096.0, A.mult)
+        ts(x("FR"), x("ZR"), 4095, A.bitwise_and)
+        tt(x("AM"), x("UX"), x("FR"), A.subtract)
+        ts(x("LA"), x("AM"), r("SC"), A.add, 7.0, A.add)
+        act(y("ZM"), y("ZA"), F.Copy, MAGIC)
+        act(y("ZI"), y("ZM"), F.Copy, -MAGIC)
+        gat("v", y("DZ"), r("ZP"), x("LA"), y("ZI"))
+        if t == STEPS - 1:
+            act(y("ZA"), y("ZM"), F.Copy, MAGIC, -1.0)
 
     def rules(t, p):
         c0, c1, chunks = PIECES[p]
@@ -275,23 +307,29 @@ def rank_program(g, core, T, topo):
         last = t == STEPS - 1
         x = lambda n: r(n, L0, L1)
         l = L0
+        pr[0] = GPR[p]
         for q, ck in chunks:
-            v, lp, hx, ab = r("D", 16 * l, 16 * (l + ck)), r("LP", l, l + ck), r("HX", 16 * l, 16 * (l + ck)), r("AB", 16 * l, 16 * (l + ck))
+            v, ab = r("D", 16 * (L0 + l), 16 * (L0 + l + ck)), r("D", 16 * (L1 + l), 16 * (L1 + l + ck))
+            lp, hx = r("LP", l, l + ck), r("HX", 16 * l, 16 * (l + ck))
             if q == "v":
                 gat("v", v, r("HD"), lp, hx)
                 na = ABS if p == NPC - 1 and l + ck == L1 else 1
                 for j in range(na):
-                    act(r("AB", ab[1] + j, ab[2], na), r("D", ab[1] + j, ab[2], na), F.Abs)
+                    act(r("D", ab[1] + j, ab[2], na), r("D", v[1] + j, v[2], na), F.Abs, 0.0, 2.0)
             else:
-                df = r(Y, 0, 16 * ck)
+                bank = X if (l - L0) // 32 % 2 else Y
                 gat("a", v, r("HD"), lp)
-                mms(df, [(r("NI"), hx), (r("ID"), v)])
-                act(ab, df, F.Abs)
+                mm(r(bank, 0, 16 * ck), r("Bh"), r("Z5", 0, 16 * ck), True, False)
+                for s in range(16):
+                    mm(r(bank, s, 16 * ck, 16), r("NI"), r(hb, l, l + ck), False, False)
+                mm(r(bank, 0, 16 * ck), r("ID"), v, False, True)
+                act(ab, r(bank, 0, 16 * ck), F.Abs, 0.0, 2.0)
             l += ck
+        pr[0] = PRI[p]
         d, y1, a2 = r(X, 0, nl), r(X, 128, 128 + nl), r(X, 0, nl)
         y0, oh, w0 = r(Y, 0, nl), r(Y, 128, 128 + nl), r(Y, 256, 256 + nl)
         k = lambda n: r(n, 0, nl)
-        mms(d, [(r("CM", 128 * s, 128 * s + 128), r("AB", 16 * L0 + s, 16 * L1, 16))
+        mms(d, [(r("CM", 128 * s, 128 * s + 128), r("D", 16 * (L0 + L1) + s, 32 * L1, 16))
                 for s in sorted(range(16), key=lambda s: s % ABS)])
         act(x("NA"), d, F.Identity, r("TB"), -8192.0)
         tt(x("NX"), d, x("NA"), A.max)
@@ -312,30 +350,38 @@ def rank_program(g, core, T, topo):
             mm(wr(sx), r("HN", 128 * s, 128 * s + 128), r("DN", L0 + s, L1, 4), False, False)
         mms(oh, [(r("DD"), x("G"))])
         for s in range(4):
+            mm(wr(se), r("H%d" % nl, 128 * s, 128 * s + 128), r("DN", L0 + s, L1, 4), False, False)
+        for s in range(4):
             mm(wr(se), r("HE", 128 * s, 128 * s + 128), r("G", L0 + s, L1, 4), False, s == 3)
         tt(x("DE"), oh, x("DZ"), A.mult)
         scan(r("ES", s0, s0 + 2 * n4), r(X, 256, 256 + 2 * n4), r("RX", s0, s0 + 2 * n4), 0.0, A.max, A.add)
-        ts(r("SL", 2 * c0, 2 * c1, 2), r("ES", sx + 3, sx + n4, 4), r("TR"), A.min)
         cp(r("EL", c0, c1), r("ES", se + 3, se + n4, 4))
+        w = DED[p]
+        if w == 1:
+            ts(r("SL", 2 * c0, 2 * c1, 2), r("ES", sx + 3, sx + n4, 4), r("TR"), A.min)
+        else:
+            ts(r("DA", 5 * c0 + 1, 5 * c1, 5), r("ES", sx + 3, sx + n4, 4), 1 / 8192, A.mult)
+            for j in range(1, w):
+                tt(r("DA", 5 * (c0 + j) + 1 + j, 5 * c1, 5), r("ES", sx + 3 + 4 * j, sx + n4, 4), r("ES", sx + 3, sx + n4 - 4 * j, 4), A.is_equal)
+            scan(r("DO", 5 * c0, 5 * c1), r("DA", 5 * c0, 5 * c1), r("DB", 5 * c0, 5 * c1), 0.0, A.add, A.min)
+            ts(r("SL", 2 * c0, c0 + c1), r("DO", 5 * c0 + 4, 5 * c1, 5), 8192.0, A.mult)
         tab, base, f = (r("YO"), "ZA", A.subtract) if last else (r("MZ"), "ZI", A.add)
-        for c in range(c1 - 1, c0 - 1, -1):
-            off, de, zi = r("SL", 2 * c, 2 * c + 1), r("DE", 16 * c, 16 * c + 16), r(base, 16 * c, 16 * c + 16)
+        for c in range(c1 - w, c0 - 1, -w):
+            o0 = 2 * c if w == 1 else c0 + c
+            off, de, zi, ze = r("SL", o0, o0 + w), r("DE", 16 * c, 16 * (c + w)), r(base, 16 * c, 16 * (c + w)), r("ZE", 0, 16 * w)
             op("v", lambda e, off=off, de=de, zi=zi: e.tensor_tensor(out=ap(tab).indirect(ap(off)), in0=ap(zi), in1=ap(de), op=f),
-               [off, de, zi], [tab], 0.05 + 16 * 3.5 * CY)
-            op("a", lambda e, off=off: e.activation(out=ap(r("NM")).indirect(ap(off)), in_=ap(r("ZE")), func=F.Silu),
-               [off, r("ZE")], [r("NM")], 0.065 + 16 * 3.5 * CY)
-        gat("a", x("DS"), r("D", 16 * L0, 16 * L1), r("EL", c0, c1))
-        gat("a", x("AD"), r("AB", 16 * L0, 16 * L1), r("EL", c0, c1))
+               [off, de, zi], [tab], 0.05 + 16 * w * 3.5 * CY)
+            op("a", lambda e, off=off, ze=ze: e.activation(out=ap(r("NM")).indirect(ap(off)), in_=ap(ze), func=F.Silu),
+               [off, ze], [r("NM")], 0.065 + 16 * w * 3.5 * CY)
+        gat("a", x("DS"), r("D", 32 * L0, 32 * L1), r("EL", c0, c1))
         mm(w0, r("Be"), x("DN"), True, False)
         l = L0
         for q, ck in chunks:
-            mm(r(Y, 256 + l - L0, 256 + l - L0 + ck), r("IH") if q == "a" else r("ID"), r(hb, l, l + ck), False, False)
+            mm(r(Y, 256 + l - L0, 256 + l - L0 + ck), r("ID") if q == "a" else r("Bf"), r(hb, l, l + ck), False, l + ck == L1)
             l += ck
-        mm(a2, r("Bf"), x("DN"), True, False)
-        mm(w0, r("IH"), x("DS"), False, True)
-        mm(a2, r("ID"), x("AD"), False, True)
-        ts(x("A1"), w0, -512.25, A.add)
-        tt(x("hn%d" % t), a2, x("A1"), A.max)
+        act(x("AD"), w0, F.Relu, r("KB"))
+        mms(a2, [(r("Bg"), k("ON")), (r("IH"), x("AD")), (r("IH"), x("DS"))])
+        ts(x("hn%d" % t), a2, MAGIC, A.add, MAGIC, A.subtract)
 
     def send(t, h):
         c0, c1 = span(PARTS[h])
@@ -345,14 +391,17 @@ def rank_program(g, core, T, topo):
 
     for t in range(STEPS):
         for h in range(len(PARTS)):
+            pr[0], tag[0] = FPR[h], "f%d" % h
             front(t, h)
-        before(t)
+        for k, part in enumerate(BEFORE):
+            pr[0], tag[0] = BPR[k], "b%d" % k
+            before(t, part)
         for h, part in enumerate(PARTS):
             for p in part:
-                pr[0] = PRI[p]
+                pr[0], tag[0] = PRI[p], "r%d" % p
                 rules(t, p)
             send(t, h)
-            pr[0] = 0.0
+            pr[0], tag[0] = 0.0, "e"
         if t < STEPS - 1:
             scan(SZ, r("NM", 0, W), r("MZ", 0, W), 0.0, A.add, A.min)
             act(r("ZP", 7, 8), r("ZP", W + 7, W + 8), F.Copy)
@@ -378,18 +427,22 @@ def covers(x, y):
     return x[3] == 1 and x[1] <= y[1] and x[2] >= y[2]
 
 
-def emit(g, T, ops, eng, sent):
+def depend(ops):
     n = len(ops)
     dep = [dict() for _ in range(n)]
-    hist = {}
+    hist, dmas = {}, {}
     for i, o in enumerate(ops):
+        if o["sem"] is not None:
+            if o["q"] in dmas:
+                dep[i][dmas[o["q"]]] = False
+            dmas[o["q"]] = i
         for wr, xs in ((False, o["rd"]), (True, o["wr"])):
             for x in xs:
                 psum = x[0][:2] == "ps"
                 for (j, y, w) in hist.get(x[0], []):
                     same = ops[j]["q"] == o["q"] and ops[j]["sem"] is None
                     if (wr or w) and meet(x, y):
-                        wait = not same or (w and not wr) or (w and WAW and o["q"] != "p")
+                        wait = not same or o["q"] != "p"
                         dep[i][j] = dep[i].get(j, False) or wait
                     elif psum:
                         dep[i][j] = dep[i].get(j, False) or not same
@@ -401,6 +454,11 @@ def emit(g, T, ops, eng, sent):
                 if x[0][:2] == "ps":
                     h[:] = [z for z in h if ops[z[0]]["q"] != o["q"] or (z[2] and o["q"] != "p")]
                 h.append((i, x, wr))
+    return dep
+
+
+def plan(ops, dep, eng):
+    n = len(ops)
     succ = [[] for _ in range(n)]
     for i in range(n):
         for j in dep[i]:
@@ -429,6 +487,39 @@ def emit(g, T, ops, eng, sent):
             if not left[k]:
                 ready[ops[k]["q"]].append(k)
         order.append(i)
+    lag = lambda j, k: ops[j]["lat"] + HOP if dep[k][j] else 0.0
+    fwd = [[(j, lag(j, i)) for j in dep[i]] for i in range(n)]
+    bwd = [[(k, lag(i, k)) for k in succ[i]] for i in range(n)]
+
+    def place_all(seq, pre, head):
+        end, busy = [0.0] * n, {q: [] for q in eng}
+        for i in seq:
+            t, d, b = max([end[j] + g0 for j, g0 in pre[i]], default=head[i]), ops[i]["dur"], busy[ops[i]["q"]]
+            lo, hi = 0, len(b)
+            while lo < hi:
+                mid = (lo + hi) // 2
+                lo, hi = (mid + 1, hi) if b[mid][1] <= t + 1e-9 else (lo, mid)
+            while lo < len(b) and b[lo][0] < t + d - 1e-9:
+                t = b[lo][1]
+                lo += 1
+            b.insert(lo, (t, t + d))
+            end[i] = t + d
+        return end
+    best, seq, zero, lats = None, order, [0.0] * n, [o["lat"] for o in ops]
+    for _ in range(ROUNDS):
+        end = place_all(seq, fwd, zero)
+        span = max(end[i] + lats[i] for i in range(n))
+        if best is None or span < best - 1e-9:
+            best, order = span, sorted(range(n), key=lambda i: (end[i] - ops[i]["dur"], i))
+        LOG.append(round(span, 1))
+        back = place_all(sorted(range(n), key=lambda i: (-end[i], -i)), bwd, lats)
+        seq = sorted(range(n), key=lambda i: (-back[i], i))
+    return order, best
+
+
+def emit(g, T, ops, eng, sent):
+    dep = depend(ops)
+    order = plan(ops, dep, eng)[0]
     count = {q: 0 for q in eng}
     mark, know, after, place = {}, {q: {} for q in eng}, {}, {}
     final = {}

@@ -2,24 +2,31 @@ import math
 from concourse.mybir import AluOpType as A, ActivationFunctionType as F
 
 N, STEPS, W, R, P = 4, 4, 2048, 4096, 256
-PIECES = [(12, 16, (("v", 32), ("a", 32))), (8, 12, (("v", 32), ("v", 32))), (4, 8, (("v", 32), ("a", 32))), (0, 4, (("v", 32), ("v", 32)))]
+_A, _V = ("a", 32), ("v", 16)
+PIECES = [(12, 16, (_V, _V, _A)), (8, 12, (_V, _V, _V, _V)), (4, 8, (_V, _V, _A)), (0, 4, (_V, _V, _V, _V))]
 PARTS = [(0, 1), (2, 3)]
 HEXP = ["agaagaagaagaagag", "agvaggavvgavagva"]
 OPEN = True
 NPC = len(PIECES)
 TW = W + 64
-DED = [4, 4, 4, 2]
+DED = [4, 4, 4, 4]
 BEFORE = [(0, 1), (2, 3)]
-BPR = [0.0, 0.0, 0.0, 0.0]
+BPR = [2.0, 0.0, 0.0, 0.0]
 BIG = float(2 ** 21)
 MAGIC = 1.5 * 2 ** 23
 HOP = 0.2
-ROUNDS = 6
+ROUNDS = 3
+LD = 0.6
+CLA = [(), (), (), ()]
+GA = [False] * 4
+DAA = [False] * 4
+TZ = False
+CUTS = [0, 2048]
 LOG = []
 PERT = {}
-PRI = [0.0, 0.0, 0.0, 0.0]
-GPR = [0.0, 0.0, 0.0, 0.0]
-FPR = [0.0, 0.0, 0.0, 0.0]
+PRI = [2.5, 2.0, 0.5, 0.0]
+GPR = [2.5, 2.0, 0.5, 0.0]
+FPR = [2.0, 2.0, 0.0, 0.0]
 PEC = 0.5
 CY = 0.83e-3
 WAW = True
@@ -30,19 +37,24 @@ SCRATCH = {
     "WT": ("sbuf", [128, 1], "bfloat16"), "TI": ("sbuf", [128, 1], "int32"),
     "YO": ("sbuf", [128, TW], "float32"), "MZ": ("sbuf", [128, TW], "float32"), "NM": ("sbuf", [128, TW], "float32"),
     "ZP": ("sbuf", [128, W + 8], "float32"), "YM": ("sbuf", [128, W], "float32"),
-    "CM": ("sbuf", [128, 2048], "bfloat16"), "SR": ("sbuf", [128, 2048], "bfloat16"),
+    "SR": ("sbuf", [128, 2048], "bfloat16"),
 }
-for _d, _w, _ns in (("float32", 1, "SC SQ TB NB SX TR QB"), ("int32", 1, "PI SI SJ"),
-                    ("bfloat16", 128, "ON B1 BO ID IH NI S1 DD BW MB OH0 I16 I128 I72 Ba Bb Bc Bd Be Bf Bg Bh"),
-                    ("float32", 16, "IK OH"), ("float32", 64, "ZE ZF"), ("float32", 80, "DA DB DO"),
-                    ("int32", 16, "UI UA UB UP UX ZR FR AM"),
-                    ("uint16", 16, "LX LA EL"), ("uint16", 32, "SL"), ("bfloat16", 512, "WU HE HN"), ("float32", 512, "DG"),
-                    ("float32", 64, "IQ RU RZ ZS RT"), ("int32", 64, "US UQ UR"), ("bfloat16", 64, "MQ VQ VN"), ("float32", 128, "JS RX ES"),
-                    ("float32", P, "ZA ZM ZI DE NA"), ("int32", P, "DZ A1 NX NN"), ("uint16", P, "LP"),
-                    ("bfloat16", P, "NP C0 C1 C2 C3 G DN DS AD"), ("bfloat16", 16 * P, "HX"), ("bfloat16", 32 * P, "D"),
-                    ("bfloat16", 512, "Z5 H32 H64 H96 H128"), ("float32", 1, "KB")):
+SUB = {}
+for _d, _w, _ns in (("float32", 1, "SC SQ SM TB NB NC SX TR QB KB K16 K15"), ("int32", 1, "PI SI SJ SK"),
+                    ("bfloat16", 128, "ON B1 BO ID IH NI S1 DD MB OH0 Ba Bb Bc Bd Be Bf Bg Bh Nx Ny Nz DP8 DN8 KM KM8 KML"),
+                    ("bfloat16", 144, "QH"), ("float32", 128, "IF"), ("float32", P, "ZB"), ("bfloat16", P, "E1 E2 E3"),
+                    ("float32", 16, "IK OH"), ("float32", 4, "OK"), ("float32", 64, "ZE ZF"), ("float32", 80, "DA DB DO"),
+                    ("int32", 16, "UX FR AM"), ("bfloat16", 144, "Q4 QW Q16"),
+                    ("uint16", 16, "LX LA EL"), ("uint16", 32, "SL"), ("float32", 512, "DG"),
+                    ("float32", 64, "IQ RU RZ RT"), ("int32", 64, "US UQ UR ZS"), ("bfloat16", 64, "VQ VN"), ("float32", 128, "JS RX ES"),
+                    ("float32", P, "ZA ZM ZI DE NA"), ("int32", P, "DZ NX NN"), ("uint16", P, "LP"),
+                    ("bfloat16", P, "NP C0 C1 C2 C3 G DN DS AD"), ("bfloat16", 16 * P, "HX"), ("bfloat16", 32 * P, "D")):
     for _n in _ns.split():
-        SCRATCH[_n] = ("sbuf", [128, _w], _d)
+        if (_d, _w) == ("bfloat16", 128):
+            SUB[_n] = 128 * len(SUB)
+        else:
+            SCRATCH[_n] = ("sbuf", [128, _w], _d)
+SCRATCH["SQM"] = ("sbuf", [128, 128 * len(SUB)], "bfloat16")
 for _b in range(8):
     SCRATCH["ps%d" % _b] = ("psum", [128, 512], "float32")
 for _t in range(STEPS + 1):
@@ -62,8 +74,11 @@ def rank_program(g, core, T, topo):
     ne = len(topo.engines(core, dst))
     eng = {"v": g.vector, "a": g.scalar, "p": g.tensor, "g": g, "s": g.sync}
     ops, pr, tag = [], [0.0], ["c"]
+    DNS = 256.0 * (PIECES[0][1] - PIECES[0][0])
 
     def r(n, lo=0, hi=None, st=1):
+        if n in SUB:
+            return ("SQM", SUB[n] + lo, SUB[n] + (128 if hi is None else hi), st)
         return (n, lo, SCRATCH[n][1][1] if hi is None else hi, st)
 
     def ap(x):
@@ -118,7 +133,8 @@ def rank_program(g, core, T, topo):
     def gat(q, o, w, off, in1=None):
         d = 0.05 + 1.5 * cnt(o) * CY
         if q == "a":
-            op("a", lambda e: e.activation(out=ap(o), in_=ap(w).indirect(ap(off)), func=F.Copy), [w, off], [o], d + 0.015)
+            op("a", lambda e: e.activation(out=ap(o), in_=ap(w).indirect(ap(off)), func=F.Copy, bias=in1 or 0.0),
+               [w, off], [o], d + 0.015)
         elif in1 is None:
             op("v", lambda e: e.tensor_scalar(out=ap(o), in0=ap(w).indirect(ap(off)), scalar1=-1.0, scalar2=None, op0=A.mult),
                [w, off], [o], d)
@@ -149,8 +165,8 @@ def rank_program(g, core, T, topo):
         op("g", lambda e: e.affine_select(out=ap(o), in_=ap(a), pattern=pat, compare_op=f, fill=fill, base=base,
                                           channel_multiplier=cm), [a], [o], 0.17 + 2 * cnt(o) * CY)
 
-    loads = [("s", "MK", "marks", None, 2.5), ("a", "hb0", "h0", None, 2.3), ("a", "WT", "w", None, 2.5)] + \
-        [("s", "OW", "owner", 512 * b, 3.5 + b) for b in range(4)] + [("s", "HD", "hdr", None, 10.6), ("a", "TI", "th", None, 3.5)]
+    loads = [("s", "MK", "marks", None, 2.2), ("a", "hb0", "h0", None, 2.2), ("a", "WT", "w", None, 2.3)] + \
+        [("s", "OW", "owner", 512 * b, 2.9 + LD * b) for b in range(4)] + [("s", "HD", "hdr", None, 2.9 + 7 * LD), ("a", "TI", "th", None, 3.0)]
     for k, (q, b, src, lo, dur) in enumerate(loads):
         pr[0] = 1000.0 - 20 * k
         if lo is None:
@@ -183,37 +199,42 @@ def rank_program(g, core, T, topo):
         tt(r("MZ", lo, hi), m, r("OW", lo, hi), A.mult)
         scan(r("ZP", 8 + lo, 8 + hi), r("NM", lo, hi), r("MZ", lo, hi), r("ZP", 7 + lo, 8 + lo) if b else 0.0, A.add, A.min)
     act(r("ZP", 7, 8), r("ZP", W + 7, W + 8), F.Copy)
-    for n in ("WU", "DG", "HE", "HN", "RU", "RZ", "RX"):
+    for n in ("Q4", "Q16", "RU", "RZ", "RX"):
         ms(r(n), 0.0)
-    for k in range(4):
-        ms(r("CM", 512 * k, 512 * k + 512), 0.0)
+    q4 = lambda n, s: r(n, 3 - s, 131 - s)
+    cp(r("Q4", 3, 131, 4), r("BO", 0, 128, 4))
+    act(r("Q16", 15, 143, 16), r("BO", 0, 128, 16), F.Copy, 0.0, 0.5)
+    ts(r("QW"), r("Q4"), r("WT"), A.mult)
     ts(r("SJ"), r("SI"), 2, A.arith_shift_right)
     cp(r("SQ"), r("SJ"))
     iota(r("IQ"), [[0, 16], [1, 4]], 0, 0)
     ts(r("VQ"), r("IQ"), r("SQ"), A.is_equal, BIG, A.mult)
-    ts(r("VN"), r("VQ"), -BIG, A.add)
+    ts(r("VN"), r("VQ"), -BIG, A.add, 16.0, A.mult)
     ms(r("RU", 3, 64, 4), -BIG)
-    ms(r("RZ", 0, 64, 4), -4 * BIG)
-    ts(r("BW"), r("BO"), r("WT"), A.mult)
+    ms(r("RZ", 0, 64, 4), -64 * BIG)
     sel(r("ID"), r("ON"), [[-1, 128]], A.is_equal, 0, 1)
+    ts(r("SK"), r("PI"), 3, A.bitwise_and)
+    cp(r("SM"), r("SK"))
+    ts(r("OK"), r("IK", 0, 4), r("SM"), A.is_equal, -4096.0, A.mult)
     for s in range(4):
-        cp(r("WU", 128 * s + s, 128 * s + 128, 4), r("BW", s, 128, 4))
-        act(r("DG", 128 * s + s, 128 * s + 128, 4), r("ID", s, 128, 4), F.Copy)
-        act(r("HE", 128 * s + s, 128 * s + 128, 4), r("BO", s, 128, 4), F.Copy, 0.0, -1.0)
-        act(r("HN", 128 * s + s, 128 * s + 128, 4), r("BO", s, 128, 4), F.Copy, 0.0, 8192.0)
-    for s in range(16):
-        act(r("CM", 128 * s + s, 128 * s + 128, 16), r("BO", 0, 128, 16), F.Copy, 0.0, 0.5)
+        act(r("DG", 128 * s, 128 * s + 128), r("ID"), F.Copy, 0.0, r("OK", s, s + 1))
     for n, src, k in (("NI", "ID", -1.0), ("IH", "ID", 0.5), ("Ba", "BO", 16.0), ("Bb", "BO", -256.0), ("Bc", "BO", 4096.0),
-                      ("Bd", "BO", -65536.0), ("Be", "BO", 512.0), ("Bf", "ID", 2.0), ("Bg", "ID", -0.25), ("Bh", "ID", 0.0)):
-        ts(r(n), r(src), k, A.mult)
-    ts(r("NB"), r("SC"), 4.0, A.mult, -4096.0, A.add)
-    ts(r("TB"), r("TI"), 8192.0, A.mult, r("NB"), A.add)
+                      ("Bd", "BO", -65536.0), ("Be", "BO", 512 / DNS), ("Bf", "ID", 2.0), ("Bg", "ID", -0.25), ("Bh", "ID", 0.0)):
+        act(r(n), r(src), F.Copy, 0.0, k)
+    ts(r("NC"), r("SC"), 4.0, A.mult, -4096.0, A.add)
+    ts(r("TB"), r("TI"), 8192.0, A.mult, r("NC"), A.add)
     ts(r("NB"), r("SC"), -16.0, A.mult)
-    ts(r("SX"), r("SC"), -BIG, A.add)
-    ts(r("TR"), r("SC"), float(W), A.add)
-    sel(r("S1"), r("ON"), [[-1, 128]], A.is_equal, 1, 1)
-    tt(r("S1"), r("S1"), r("BO"), A.mult)
-    tt(r("DD"), r("ID"), r("S1"), A.subtract)
+    ts(r("SX"), r("SC"), -BIG * 4096 / DNS, A.add)
+    ts(r("TR"), r("SC"), float(W), A.add, DNS / 4096, A.mult)
+    sel(r("S1"), r("BO"), [[-1, 128]], A.is_equal, 1, 1)
+    tt(r("S1"), r("ID"), r("S1"), A.subtract)
+    for n, src, k in (("DD", "S1", 0.5), ("DP8", "S1", 4096.0), ("DN8", "S1", -4096.0), ("QH", "Q4", -0.5), ("IF", "ID", 1.0),
+                      ("KM", "ID", -MAGIC), ("KM8", "ID", -MAGIC - 8192 * 8), ("KML", "ID", -MAGIC + 8192 * 8),
+                      ("Nx", "BO", -16.0), ("Ny", "BO", 256.0), ("Nz", "BO", -4096.0)):
+        if (TZ or n in ("DD", "QH") or n[0] == "N") and (n[0] != "N" or any(CLA)):
+            act(r(n), r(src), F.Copy, 0.0, k * (8 if n[1:] in ("P8", "N8") else 1))
+    ms(r("K16"), -16.0)
+    ms(r("K15"), 15.5)
     iota(r("JS"), [[0, 8], [1, 16]], 0, 0)
     ts(r("OH0"), r("JS"), r("SC"), A.is_equal)
     ms(r("ZF"), 8192.0)
@@ -236,14 +257,10 @@ def rank_program(g, core, T, topo):
     iota(r("RT", 0, 16), [[256, 16]], 16, 0)
     ts(r("RT", 16, 17), r("SC"), 16.0, A.mult, -BIG, A.add)
     for p, (c0, c1, _c) in enumerate(PIECES):
-        ts(r("RX", at[p][1] + 3, at[p][1] + 4 * (c1 - c0), 4), r("RT", 0, c1 - c0), r("RT", 16, 17), A.add, 256.0 * (c1 - c0), A.add)
-    for nl in sorted(set(16 * (c1 - c0) for c0, c1, _c in PIECES)):
-        ms(r("H%d" % nl), 0.0)
-        for s in range(4):
-            act(r("H%d" % nl, 128 * s + s, 128 * s + 128, 4), r("BO", s, 128, 4), F.Copy, 0.0, -16.0 * nl)
+        ts(r("RX", at[p][1] + 3, at[p][1] + 4 * (c1 - c0), 4), r("RT", 0, c1 - c0), r("RT", 16, 17), A.add,
+           -8.0 if GA[p] else 0.0, A.add)
     iota(r("UQ"), [[0, 16], [2, 4]], 0, 0)
     ms(r("KB"), -512.0)
-    ms(r("Z5"), 0.0)
 
     SZ = r("ZP", 8, 8 + W)
 
@@ -255,7 +272,7 @@ def rank_program(g, core, T, topo):
         L0, L1, n4 = 16 * c0, 16 * c1, 4 * (c1 - c0)
         hb, u = "hb%d" % t, r("ps%d" % (2 * PARTS[h][0]), 448, 448 + n4)
         x = lambda n: r(n, c0, c1)
-        mms(u, [(r("ID"), r("VQ", 0, n4))] + [(r("WU", 128 * s, 128 * s + 128), r(hb, L0 + s, L1, 4)) for s in range(4)])
+        mms(u, [(r("ID"), r("VQ", 0, n4))] + [(q4("QW", s), r(hb, L0 + s, L1, 4)) for s in range(4)])
         scan(r("US", 4 * c0, 4 * c1), u, r("RU", 0, n4), 0.0, A.max, A.add)
         ts(r("UQ", 4 * c0 + 3, 4 * c1, 4), r("US", 4 * c0 + 3, 4 * c1, 4), 4095, A.bitwise_and)
         scan(r("UR", 4 * c0, 4 * c1), r("UQ", 4 * c0, 4 * c1), r("UQ", 4 * c0, 4 * c1), 0.0, A.add, A.mult)
@@ -265,7 +282,7 @@ def rank_program(g, core, T, topo):
             if pair[0] in PARTS[h]:
                 a0, a1 = span(pair)
                 lo = min(at[p][2] for p in pair)
-                ts(r("RX", lo + 3, lo + 4 * (a1 - a0), 4), r("UX", a0, a1), r("SX"), A.add)
+                ts(r("RX", lo + 3, lo + 4 * (a1 - a0), 4), r("UX", a0, a1), r("SX"), A.add, DNS / 4096, A.mult)
         vs = []
         for p in PARTS[h]:
             l = 16 * PIECES[p][0]
@@ -290,11 +307,13 @@ def rank_program(g, core, T, topo):
         gat("a", y("ZA"), SZ, x("LX"))
         mms(zw, [(r("ID"), r("VN", 0, n4))] + [(r("DG", 128 * s, 128 * s + 128), r("ZA", 16 * c0 + s, 16 * c1, 4)) for s in range(4)])
         scan(r("ZS", 4 * c0, 4 * c1), r("RZ", 0, n4), zw, 0.0, A.add, A.max)
-        ts(x("ZR"), r("ZS", 4 * c0 + 3, 4 * c1, 4), -4096.0, A.mult)
-        ts(x("FR"), x("ZR"), 4095, A.bitwise_and)
+        ts(x("FR"), r("ZS", 4 * c0 + 3, 4 * c1, 4), 4095, A.bitwise_and)
         tt(x("AM"), x("UX"), x("FR"), A.subtract)
         ts(x("LA"), x("AM"), r("SC"), A.add, 7.0, A.add)
         act(y("ZM"), y("ZA"), F.Copy, MAGIC)
+        if TZ:
+            gat("a", y("ZB"), r("ZP"), x("LA"), MAGIC)
+            return
         act(y("ZI"), y("ZM"), F.Copy, -MAGIC)
         gat("v", y("DZ"), r("ZP"), x("LA"), y("ZI"))
         if t == STEPS - 1:
@@ -309,7 +328,7 @@ def rank_program(g, core, T, topo):
         l = L0
         pr[0] = GPR[p]
         for q, ck in chunks:
-            v, ab = r("D", 16 * (L0 + l), 16 * (L0 + l + ck)), r("D", 16 * (L1 + l), 16 * (L1 + l + ck))
+            ab, v = r("D", 16 * (L0 + l), 16 * (L0 + l + ck)), r("D", 16 * (L1 + l), 16 * (L1 + l + ck))
             lp, hx = r("LP", l, l + ck), r("HX", 16 * l, 16 * (l + ck))
             if q == "v":
                 gat("v", v, r("HD"), lp, hx)
@@ -319,7 +338,7 @@ def rank_program(g, core, T, topo):
             else:
                 bank = X if (l - L0) // 32 % 2 else Y
                 gat("a", v, r("HD"), lp)
-                mm(r(bank, 0, 16 * ck), r("Bh"), r("Z5", 0, 16 * ck), True, False)
+                mm(r(bank, 0, 16 * ck), r("Bh"), r("SR", 0, 16 * ck), True, False)
                 for s in range(16):
                     mm(r(bank, s, 16 * ck, 16), r("NI"), r(hb, l, l + ck), False, False)
                 mm(r(bank, 0, 16 * ck), r("ID"), v, False, True)
@@ -329,43 +348,71 @@ def rank_program(g, core, T, topo):
         d, y1, a2 = r(X, 0, nl), r(X, 128, 128 + nl), r(X, 0, nl)
         y0, oh, w0 = r(Y, 0, nl), r(Y, 128, 128 + nl), r(Y, 256, 256 + nl)
         k = lambda n: r(n, 0, nl)
-        mms(d, [(r("CM", 128 * s, 128 * s + 128), r("D", 16 * (L0 + L1) + s, 32 * L1, 16))
+        mms(d, [(r("Q16", 15 - s, 143 - s), r("D", 32 * L0 + s, 16 * (L0 + L1), 16))
                 for s in sorted(range(16), key=lambda s: s % ABS)])
         act(x("NA"), d, F.Identity, r("TB"), -8192.0)
         tt(x("NX"), d, x("NA"), A.max)
         ts(x("NN"), x("NX"), 2, A.arith_shift_right, 15, A.bitwise_and)
         ts(x("NP"), x("NN"), r("NB"), A.add)
-        tt(x("C0"), x("NN"), k("OH0"), A.mult)
+        mms(oh, [(r("ID"), k("OH0"))])
+        tt(x("C0"), oh, x("NN"), A.mult)
         for j in range(1, 5):
             y = y1 if j % 2 else y0
-            mms(y, [(r("ID"), x("NP"))] + [(r("B" + "abcd"[j - 1 - i]), x("C%d" % i)) for i in range(j)])
-            if j < 4:
+            terms = [(r("ID"), x("NP"))]
+            for i in range(j):
+                terms.append((r("B" + "abcd"[j - 1 - i]), x("C%d" % i)))
+                if i in CLA[p]:
+                    terms.append((r("N" + "xyz"[j - 1 - i]), x("E%d" % i)))
+            mms(y, terms)
+            if j == 4 and GA[p]:
+                mms(y1, terms)
+            if j in CLA[p]:
+                act(x("C%d" % j), y, F.Relu)
+                act(x("E%d" % j), y, F.Relu, r("K16"))
+            elif j < 4:
                 ts(x("C%d" % j), y, 0.0, A.max, 16.0, A.min)
+        if GA[p]:
+            act(x("G"), y1, F.Sign, r("K15"), -1.0)
         s0, se, sx = at[p]
         wr = lambda a: r(X, 256 + a - s0, 256 + a - s0 + n4)
         mm(r(X, 256, 256 + 2 * n4), r("ID"), r("VQ", 0, 2 * n4), True, False)
-        ts(x("DN"), y0, r("SC"), A.is_equal)
-        ts(x("G"), y0, 16.0, A.is_lt)
+        ts(x("DN"), y0, r("SC"), A.is_equal, DNS, A.mult)
+        if not GA[p]:
+            ts(x("G"), y0, 16.0, A.is_lt, 2.0, A.mult)
+        for a in (sx, se):
+            for s in range(4):
+                mm(wr(a), q4("Q4", s), r("DN", L0 + s, L1, 4), False, False)
         for s in range(4):
-            mm(wr(sx), r("HN", 128 * s, 128 * s + 128), r("DN", L0 + s, L1, 4), False, False)
-        mms(oh, [(r("DD"), x("G"))])
-        for s in range(4):
-            mm(wr(se), r("H%d" % nl, 128 * s, 128 * s + 128), r("DN", L0 + s, L1, 4), False, False)
-        for s in range(4):
-            mm(wr(se), r("HE", 128 * s, 128 * s + 128), r("G", L0 + s, L1, 4), False, s == 3)
-        tt(x("DE"), oh, x("DZ"), A.mult)
+            mm(wr(se), q4("QH", s), r("G", L0 + s, L1, 4), False, s == 3)
+        one = [(r("DD"), k("ON"))] if GA[p] else []
+        if TZ:
+            pos, neg = ("DN8", "DP8") if last else ("DP8", "DN8")
+            on = lambda n: [(r(n), k("ON"))] if GA[p] else []
+            t1, t2 = r(Y, 128, 128 + nl), r(Y, 384, 384 + nl)
+            mms(t1, [(r("KML" if last else "KM8"), k("ON")), (r("IF"), x("ZB"))] + on(pos) + [(r(pos), x("G"))])
+            mms(t2, [(r("KM"), k("ON")), (r("IF"), x("ZM"))] + on(neg) + [(r(neg), x("G"))])
+            act(x("DE"), t1, F.Copy, 0.0, -1.0 if last else 1.0)
+            act(x("ZI"), t2, F.Copy, 0.0, -1.0 if last else 1.0)
+        else:
+            mms(oh, one + [(r("DD"), x("G"))])
+            tt(x("DE"), oh, x("DZ"), A.mult)
         scan(r("ES", s0, s0 + 2 * n4), r(X, 256, 256 + 2 * n4), r("RX", s0, s0 + 2 * n4), 0.0, A.max, A.add)
         cp(r("EL", c0, c1), r("ES", se + 3, se + n4, 4))
         w = DED[p]
         if w == 1:
-            ts(r("SL", 2 * c0, 2 * c1, 2), r("ES", sx + 3, sx + n4, 4), r("TR"), A.min)
+            ts(r("SL", 2 * c0, 2 * c1, 2), r("ES", sx + 3, sx + n4, 4), r("TR"), A.min, 4096 / DNS, A.mult)
         else:
-            ts(r("DA", 5 * c0 + 1, 5 * c1, 5), r("ES", sx + 3, sx + n4, 4), 1 / 8192, A.mult)
+            if DAA[p]:
+                act(r("DA", 5 * c0 + 1, 5 * c1, 5), r("ES", sx + 3, sx + n4, 4), F.Copy, 0.0, 0.5 / DNS)
+            else:
+                ts(r("DA", 5 * c0 + 1, 5 * c1, 5), r("ES", sx + 3, sx + n4, 4), 0.5 / DNS, A.mult)
             for j in range(1, w):
                 tt(r("DA", 5 * (c0 + j) + 1 + j, 5 * c1, 5), r("ES", sx + 3 + 4 * j, sx + n4, 4), r("ES", sx + 3, sx + n4 - 4 * j, 4), A.is_equal)
             scan(r("DO", 5 * c0, 5 * c1), r("DA", 5 * c0, 5 * c1), r("DB", 5 * c0, 5 * c1), 0.0, A.add, A.min)
             ts(r("SL", 2 * c0, c0 + c1), r("DO", 5 * c0 + 4, 5 * c1, 5), 8192.0, A.mult)
         tab, base, f = (r("YO"), "ZA", A.subtract) if last else (r("MZ"), "ZI", A.add)
+        if TZ:
+            base, f = "ZI", A.max
         for c in range(c1 - w, c0 - 1, -w):
             o0 = 2 * c if w == 1 else c0 + c
             off, de, zi, ze = r("SL", o0, o0 + w), r("DE", 16 * c, 16 * (c + w)), r(base, 16 * c, 16 * (c + w)), r("ZE", 0, 16 * w)
@@ -403,7 +450,8 @@ def rank_program(g, core, T, topo):
             send(t, h)
             pr[0], tag[0] = 0.0, "e"
         if t < STEPS - 1:
-            scan(SZ, r("NM", 0, W), r("MZ", 0, W), 0.0, A.add, A.min)
+            for lo, hi in zip(CUTS, CUTS[1:]):
+                scan(r("ZP", 8 + lo, 8 + hi), r("NM", lo, hi), r("MZ", lo, hi), r("ZP", 7 + lo, 8 + lo) if lo else 0.0, A.add, A.min)
             act(r("ZP", 7, 8), r("ZP", W + 7, W + 8), F.Copy)
         if t == STEPS - 2:
             for lo in range(0, W, 512):

import math
from concourse.mybir import AluOpType as A, ActivationFunctionType as F

N, STEPS, W, R, P = 4, 4, 2048, 4096, 256
_A, _V = ("a", 32), ("v", 16)
PIECES = [(12, 16, (_V, _V, _A)), (8, 12, (_V, _V, _V, _V)), (4, 8, (_V, _V, _A)), (0, 4, (_V, _V, _V, _V))]
PARTS = [(0, 1), (2, 3)]
HEXP = ["agaagaagaagaagag", "agvaggavvgavagva"]
OPEN = True
NPC = len(PIECES)
TW = W + 64
DED = [4, 4, 4, 4]
BEFORE = [(0, 1), (2, 3)]
BPR = [2.0, 0.0, 0.0, 0.0]
BIG = float(2 ** 21)
MAGIC = 1.5 * 2 ** 23
HOP = 0.2
ROUNDS = 3
LD = 0.6
CLA = [(), (), (), ()]
GA = [False] * 4
DAA = [False] * 4
TZ = False
CUTS = [0, 2048]
LOG = []
PERT = {}
PRI = [2.5, 2.0, 0.5, 0.0]
GPR = [2.5, 2.0, 0.5, 0.0]
FPR = [2.0, 2.0, 0.0, 0.0]
PEC = 0.5
CY = 0.83e-3
WAW = True
ABS = 1

SCRATCH = {
    "HD": ("sbuf", [128, R], "bfloat16"), "OW": ("sbuf", [128, W], "int32"), "MK": ("sbuf", [128, 128], "int32"),
    "WT": ("sbuf", [128, 1], "bfloat16"), "TI": ("sbuf", [128, 1], "int32"),
    "YO": ("sbuf", [128, TW], "float32"), "MZ": ("sbuf", [128, TW], "float32"), "NM": ("sbuf", [128, TW], "float32"),
    "ZP": ("sbuf", [128, W + 8], "float32"), "YM": ("sbuf", [128, W], "float32"),
    "SR": ("sbuf", [128, 2048], "bfloat16"),
}
SUB = {}
for _d, _w, _ns in (("float32", 1, "SC SQ SM TB NB NC SX TR QB KB K16 K15"), ("int32", 1, "PI SI SJ SK"),
                    ("bfloat16", 128, "ON B1 BO ID IH NI S1 DD MB OH0 Ba Bb Bc Bd Be Bf Bg Bh Nx Ny Nz DP8 DN8 KM KM8 KML"),
                    ("bfloat16", 144, "QH"), ("float32", 128, "IF"), ("float32", P, "ZB"), ("bfloat16", P, "E1 E2 E3"),
                    ("float32", 16, "IK OH"), ("float32", 4, "OK"), ("float32", 64, "ZE ZF"), ("float32", 80, "DA DB DO"),
                    ("int32", 16, "UX FR AM"), ("bfloat16", 144, "Q4 QW Q16"),
                    ("uint16", 16, "LX LA EL"), ("uint16", 32, "SL"), ("float32", 512, "DG"),
                    ("float32", 64, "IQ RU RZ RT"), ("int32", 64, "US UQ UR ZS"), ("bfloat16", 64, "VQ VN"), ("float32", 128, "JS RX ES"),
                    ("float32", P, "ZA ZM ZI DE NA"), ("int32", P, "DZ NX NN"), ("uint16", P, "LP"),
                    ("bfloat16", P, "NP C0 C1 C2 C3 G DN DS AD"), ("bfloat16", 16 * P, "HX"), ("bfloat16", 32 * P, "D")):
    for _n in _ns.split():
        if (_d, _w) == ("bfloat16", 128):
            SUB[_n] = 128 * len(SUB)
        else:
            SCRATCH[_n] = ("sbuf", [128, _w], _d)
SCRATCH["SQM"] = ("sbuf", [128, 128 * len(SUB)], "bfloat16")
for _b in range(8):
    SCRATCH["ps%d" % _b] = ("psum", [128, 512], "float32")
for _t in range(STEPS + 1):
    SCRATCH["hb%d" % _t] = ("sbuf", [128, P], "bfloat16")
    SCRATCH["hn%d" % _t] = ("sbuf", [128, P], "bfloat16")
SEMAPHORES = ["qv", "qa", "qp", "qg", "ls"] + ["dm%d" % k for k in range(24)] + \
    ["ar%d_%d" % (t, h) for t in range(1, STEPS + 1) for h in range(4)]


def rank_program(g, core, T, topo):
    rank = T.rank_of(core)
    if rank is None:
        return
    dst = T.cores[(rank + 1) % N]
    rid, pid, _e = topo.addr(dst)
    mask = topo.mask(core, dst)
    ne = len(topo.engines(core, dst))
    eng = {"v": g.vector, "a": g.scalar, "p": g.tensor, "g": g, "s": g.sync}
    ops, pr, tag = [], [0.0], ["c"]
    DNS = 256.0 * (PIECES[0][1] - PIECES[0][0])

    def r(n, lo=0, hi=None, st=1):
        if n in SUB:
            return ("SQM", SUB[n] + lo, SUB[n] + (128 if hi is None else hi), st)
        return (n, lo, SCRATCH[n][1][1] if hi is None else hi, st)

    def ap(x):
        if not isinstance(x, tuple):
            return x
        b, lo, hi, st = x
        if SCRATCH[b][1][0] == 2:
            return T[b][0:2, lo:hi]
        return T[b][:, lo:hi] if st == 1 else T[b][:, lo:hi:st]

    def cnt(x):
        return -(-(x[2] - x[1]) // x[3])

    def ps(x):
        return isinstance(x, tuple) and x[0][:2] == "ps"

    def two(*xs):
        return all(SCRATCH[x[0]][2] in ("bfloat16", "uint16") for x in xs)

    def op(q, fn, rd, wr, dur, sem=None, lat=0.0):
        ops.append({"q": q, "fn": fn, "rd": [x for x in rd if isinstance(x, tuple)], "wr": wr, "dur": dur,
                    "sem": sem, "lat": lat, "pr": pr[0] + PERT.get((q, wr[0][0][:3] if wr else "", tag[0]), 0.0),
                    "key": (q, wr[0][0][:3] if wr else "", tag[0])})

    def tt(o, a, b, f):
        c = cnt(o) * (1 if ps(a) or ps(b) else 2)
        op("v", lambda e: e.tensor_tensor(out=ap(o), in0=ap(a), in1=ap(b), op=f), [a, b], [o], max(64, c) * CY)

    def ts(o, a, s1, f0, s2=None, f1=None):
        c = cnt(o) * (0.5 if two(o, a) else 1)
        if f1 is None:
            fn = lambda e: e.tensor_scalar(out=ap(o), in0=ap(a), scalar1=ap(s1), scalar2=None, op0=f0)
        else:
            fn = lambda e: e.tensor_scalar(out=ap(o), in0=ap(a), scalar1=ap(s1), scalar2=ap(s2), op0=f0, op1=f1)
        op("v", fn, [a, s1, s2], [o], max(64, c) * CY)

    def cp(o, a):
        c = cnt(o) * (0.5 if two(o, a) else 1)
        op("v", lambda e: e.tensor_copy(out=ap(o), in_=ap(a)), [a], [o], max(64, c) * CY)

    def scan(o, a, b, ini, o0, o1):
        op("v", lambda e: e.tensor_tensor_scan(out=ap(o), data0=ap(a), data1=ap(b), initial=ap(ini), op0=o0, op1=o1),
           [a, b, ini], [o], max(64, cnt(o)) * CY)

    def ms(o, k):
        op("v", lambda e: e.memset(ap(o), k), [], [o], max(64, cnt(o) * (0.5 if two(o) else 1)) * CY)

    def act(o, a, f, bias=0.0, scale=1.0, more=0.0):
        op("a", lambda e: e.activation(out=ap(o), in_=ap(a), func=f, bias=ap(bias), scale=ap(scale)), [a, bias, scale], [o],
           max(64, cnt(o)) * CY + more)

    def gat(q, o, w, off, in1=None):
        d = 0.05 + 1.5 * cnt(o) * CY
        if q == "a":
            op("a", lambda e: e.activation(out=ap(o), in_=ap(w).indirect(ap(off)), func=F.Copy, bias=in1 or 0.0),
               [w, off], [o], d + 0.015)
        elif in1 is None:
            op("v", lambda e: e.tensor_scalar(out=ap(o), in0=ap(w).indirect(ap(off)), scalar1=-1.0, scalar2=None, op0=A.mult),
               [w, off], [o], d)
        else:
            op("v", lambda e: e.tensor_tensor(out=ap(o), in0=ap(w).indirect(ap(off)), in1=ap(in1), op=A.subtract),
               [w, off, in1], [o], d)

    def mm(o, l, x, start, stop):
        op("p", lambda e: e.matmul(ap(o), ap(l), ap(x), start, stop), [l, x], [o],
           max(64, cnt(o)) * CY * PEC * (4 if SCRATCH[x[0]][2] == "float32" else 1))

    def mms(o, pairs, start=True, stop=True):
        for k, (l, x) in enumerate(pairs):
            mm(o, l, x, start and k == 0, (stop or not OPEN) and k == len(pairs) - 1)

    ndma = [0]

    def dma(q, o_fn, i_fn, rd, wr, dur):
        s = "dm%d" % ndma[0]
        ndma[0] += 1
        op(q, lambda e: e.dma_start(out=o_fn(), in_=i_fn()), rd, wr, 0.06, sem=(s, 16), lat=dur)

    def iota(o, pat, base, cm):
        op("g", lambda e: e.iota(ap(o), pat, base, cm, allow_small_or_imprecise_dtypes=True), [], [o],
           0.13 + 2 * cnt(o) * CY)

    def sel(o, a, pat, f, base, cm, fill=0.0):
        op("g", lambda e: e.affine_select(out=ap(o), in_=ap(a), pattern=pat, compare_op=f, fill=fill, base=base,
                                          channel_multiplier=cm), [a], [o], 0.17 + 2 * cnt(o) * CY)

    loads = [("s", "MK", "marks", None, 2.2), ("a", "hb0", "h0", None, 2.2), ("a", "WT", "w", None, 2.3)] + \
        [("s", "OW", "owner", 512 * b, 2.9 + LD * b) for b in range(4)] + [("s", "HD", "hdr", None, 2.9 + 7 * LD), ("a", "TI", "th", None, 3.0)]
    for k, (q, b, src, lo, dur) in enumerate(loads):
        pr[0] = 1000.0 - 20 * k
        if lo is None:
            dma(q, lambda b=b: T[b][:], lambda src=src: T[src][:], [], [r(b)], dur)
        else:
            dma(q, lambda lo=lo: T.OW[:, lo:lo + 512], lambda lo=lo: T.owner[:, lo:lo + 512], [], [r("OW", lo, lo + 512)], dur)
    pr[0] = 0.0

    iota(r("PI"), [[0, 1]], 0, 1)
    ms(r("ON"), 1.0)
    ts(r("SI"), r("PI"), 15, A.bitwise_and)
    cp(r("SC"), r("SI"))
    sel(r("B1"), r("ON"), [[-16, 8], [0, 16]], A.is_ge, 0, 1)
    sel(r("BO"), r("B1"), [[16, 8], [0, 16]], A.is_ge, 15, -1)
    iota(r("IK"), [[1, 16]], 0, 0)
    ts(r("OH"), r("IK"), r("SC"), A.is_equal)
    for k in range(16):
        if k % 2:
            act(r("SR", 128 * k, 128 * k + 128), r("BO"), F.Copy, 0.0, r("OH", k, k + 1))
        else:
            ts(r("SR", 128 * k, 128 * k + 128), r("BO"), r("OH", k, k + 1), A.mult)
    ts(r("MB"), r("MK"), -2.0, A.mult, 1.0, A.add)
    ms(r("ZP", 0, 8), 0.0)
    for b in range(4):
        lo, hi = 512 * b, 512 * b + 512
        for k in range(4 * b, 4 * b + 4):
            mm(r("ps%d" % b, 128 * (k % 4), 128 * (k % 4) + 128), r("SR", 128 * k, 128 * k + 128), r("MB"), True, True)
        m = r("ps%d" % b)
        act(r("NM", lo, hi), m, F.Copy, 2048.0, -2048.0 - 1 / 4096)
        tt(r("MZ", lo, hi), m, r("OW", lo, hi), A.mult)
        scan(r("ZP", 8 + lo, 8 + hi), r("NM", lo, hi), r("MZ", lo, hi), r("ZP", 7 + lo, 8 + lo) if b else 0.0, A.add, A.min)
    act(r("ZP", 7, 8), r("ZP", W + 7, W + 8), F.Copy)
    for n in ("Q4", "Q16", "RU", "RZ", "RX"):
        ms(r(n), 0.0)
    q4 = lambda n, s: r(n, 3 - s, 131 - s)
    cp(r("Q4", 3, 131, 4), r("BO", 0, 128, 4))
    act(r("Q16", 15, 143, 16), r("BO", 0, 128, 16), F.Copy, 0.0, 0.5)
    ts(r("QW"), r("Q4"), r("WT"), A.mult)
    ts(r("SJ"), r("SI"), 2, A.arith_shift_right)
    cp(r("SQ"), r("SJ"))
    iota(r("IQ"), [[0, 16], [1, 4]], 0, 0)
    ts(r("VQ"), r("IQ"), r("SQ"), A.is_equal, BIG, A.mult)
    ts(r("VN"), r("VQ"), -BIG, A.add, 16.0, A.mult)
    ms(r("RU", 3, 64, 4), -BIG)
    ms(r("RZ", 0, 64, 4), -64 * BIG)
    sel(r("ID"), r("ON"), [[-1, 128]], A.is_equal, 0, 1)
    ts(r("SK"), r("PI"), 3, A.bitwise_and)
    cp(r("SM"), r("SK"))
    ts(r("OK"), r("IK", 0, 4), r("SM"), A.is_equal, -4096.0, A.mult)
    for s in range(4):
        act(r("DG", 128 * s, 128 * s + 128), r("ID"), F.Copy, 0.0, r("OK", s, s + 1))
    for n, src, k in (("NI", "ID", -1.0), ("IH", "ID", 0.5), ("Ba", "BO", 16.0), ("Bb", "BO", -256.0), ("Bc", "BO", 4096.0),
                      ("Bd", "BO", -65536.0), ("Be", "BO", 512 / DNS), ("Bf", "ID", 2.0), ("Bg", "ID", -0.25), ("Bh", "ID", 0.0)):
        act(r(n), r(src), F.Copy, 0.0, k)
    ts(r("NC"), r("SC"), 4.0, A.mult, -4096.0, A.add)
    ts(r("TB"), r("TI"), 8192.0, A.mult, r("NC"), A.add)
    ts(r("NB"), r("SC"), -16.0, A.mult)
    ts(r("SX"), r("SC"), -BIG * 4096 / DNS, A.add)
    ts(r("TR"), r("SC"), float(W), A.add, DNS / 4096, A.mult)
    sel(r("S1"), r("BO"), [[-1, 128]], A.is_equal, 1, 1)
    tt(r("S1"), r("ID"), r("S1"), A.subtract)
    for n, src, k in (("DD", "S1", 0.5), ("DP8", "S1", 4096.0), ("DN8", "S1", -4096.0), ("QH", "Q4", -0.5), ("IF", "ID", 1.0),
                      ("KM", "ID", -MAGIC), ("KM8", "ID", -MAGIC - 8192 * 8), ("KML", "ID", -MAGIC + 8192 * 8),
                      ("Nx", "BO", -16.0), ("Ny", "BO", 256.0), ("Nz", "BO", -4096.0)):
        if (TZ or n in ("DD", "QH") or n[0] == "N") and (n[0] != "N" or any(CLA)):
            act(r(n), r(src), F.Copy, 0.0, k * (8 if n[1:] in ("P8", "N8") else 1))
    ms(r("K16"), -16.0)
    ms(r("K15"), 15.5)
    iota(r("JS"), [[0, 8], [1, 16]], 0, 0)
    ts(r("OH0"), r("JS"), r("SC"), A.is_equal)
    ms(r("ZF"), 8192.0)
    act(r("ZE"), r("ZF"), F.Silu, more=1.3)
    ms(r("QB"), 1 / 4096)
    at = {}
    pairs = [part[k:k + 2] for part in PARTS for k in range(0, len(part), 2)]
    ms(r("DA"), 0.0)
    ms(r("DB"), 4.0)
    ms(r("DB", 0, 80, 5), 0.0)
    iota(r("RT", 32, 48), [[0, 4], [16, 4]], W, 0)
    ts(r("DB", 4, 80, 5), r("RT", 32, 48), r("SC"), A.add, 1 / 8192, A.mult)
    for part in pairs:
        cs = sorted(part, key=lambda p: PIECES[p][0])
        lo = 8 * PIECES[cs[0]][0]
        for k, p in enumerate(cs):
            n4 = 4 * (PIECES[p][1] - PIECES[p][0])
            at[p] = (lo, lo, lo + n4) if k == 0 else (lo, lo + n4, lo)
            lo += 2 * n4
    iota(r("RT", 0, 16), [[256, 16]], 16, 0)
    ts(r("RT", 16, 17), r("SC"), 16.0, A.mult, -BIG, A.add)
    for p, (c0, c1, _c) in enumerate(PIECES):
        ts(r("RX", at[p][1] + 3, at[p][1] + 4 * (c1 - c0), 4), r("RT", 0, c1 - c0), r("RT", 16, 17), A.add,
           -8.0 if GA[p] else 0.0, A.add)
    iota(r("UQ"), [[0, 16], [2, 4]], 0, 0)
    ms(r("KB"), -512.0)

    SZ = r("ZP", 8, 8 + W)

    def span(part):
        return min(PIECES[p][0] for p in part), max(PIECES[p][1] for p in part)

    def front(t, h):
        c0, c1 = span(PARTS[h])
        L0, L1, n4 = 16 * c0, 16 * c1, 4 * (c1 - c0)
        hb, u = "hb%d" % t, r("ps%d" % (2 * PARTS[h][0]), 448, 448 + n4)
        x = lambda n: r(n, c0, c1)
        mms(u, [(r("ID"), r("VQ", 0, n4))] + [(q4("QW", s), r(hb, L0 + s, L1, 4)) for s in range(4)])
        scan(r("US", 4 * c0, 4 * c1), u, r("RU", 0, n4), 0.0, A.max, A.add)
        ts(r("UQ", 4 * c0 + 3, 4 * c1, 4), r("US", 4 * c0 + 3, 4 * c1, 4), 4095, A.bitwise_and)
        scan(r("UR", 4 * c0, 4 * c1), r("UQ", 4 * c0, 4 * c1), r("UQ", 4 * c0, 4 * c1), 0.0, A.add, A.mult)
        ts(x("UX"), r("UR", 4 * c0 + 3, 4 * c1, 4), 5, A.arith_shift_right, 2032, A.bitwise_and)
        ts(x("LX"), x("UX"), r("SC"), A.add)
        for pair in pairs:
            if pair[0] in PARTS[h]:
                a0, a1 = span(pair)
                lo = min(at[p][2] for p in pair)
                ts(r("RX", lo + 3, lo + 4 * (a1 - a0), 4), r("UX", a0, a1), r("SX"), A.add, DNS / 4096, A.mult)
        vs = []
        for p in PARTS[h]:
            l = 16 * PIECES[p][0]
            for q, ck in PIECES[p][2]:
                vs += [l, l + ck] if q == "v" else []
                l += ck
        for s in range(16 if vs else 0):
            o, i = r("HX", 16 * min(vs) + s, 16 * max(vs), 16), r(hb, min(vs), max(vs))
            if HEXP[h][s] == "a":
                act(o, i, F.Copy)
            elif HEXP[h][s] == "v":
                cp(o, i)
            else:
                sel(o, i, [[0, cnt(i)]], A.is_gt, 1, 0)
        gat("v", r("LP", L0, L1), SZ, x("LX"))

    def before(t, part):
        c0, c1 = span(part)
        n4 = 4 * (c1 - c0)
        zw = r("ps%d" % (2 * part[-1]), 384, 384 + n4)
        x, y = lambda n: r(n, c0, c1), lambda n: r(n, 16 * c0, 16 * c1)
        gat("a", y("ZA"), SZ, x("LX"))
        mms(zw, [(r("ID"), r("VN", 0, n4))] + [(r("DG", 128 * s, 128 * s + 128), r("ZA", 16 * c0 + s, 16 * c1, 4)) for s in range(4)])
        scan(r("ZS", 4 * c0, 4 * c1), r("RZ", 0, n4), zw, 0.0, A.add, A.max)
        ts(x("FR"), r("ZS", 4 * c0 + 3, 4 * c1, 4), 4095, A.bitwise_and)
        tt(x("AM"), x("UX"), x("FR"), A.subtract)
        ts(x("LA"), x("AM"), r("SC"), A.add, 7.0, A.add)
        act(y("ZM"), y("ZA"), F.Copy, MAGIC)
        if TZ:
            gat("a", y("ZB"), r("ZP"), x("LA"), MAGIC)
            return
        act(y("ZI"), y("ZM"), F.Copy, -MAGIC)
        gat("v", y("DZ"), r("ZP"), x("LA"), y("ZI"))
        if t == STEPS - 1:
            act(y("ZA"), y("ZM"), F.Copy, MAGIC, -1.0)

    def rules(t, p):
        c0, c1, chunks = PIECES[p]
        nl, n4, L0, L1 = 16 * (c1 - c0), 4 * (c1 - c0), 16 * c0, 16 * c1
        hb, X, Y = "hb%d" % t, "ps%d" % (2 * p), "ps%d" % (2 * p + 1)
        last = t == STEPS - 1
        x = lambda n: r(n, L0, L1)
        l = L0
        pr[0] = GPR[p]
        for q, ck in chunks:
            ab, v = r("D", 16 * (L0 + l), 16 * (L0 + l + ck)), r("D", 16 * (L1 + l), 16 * (L1 + l + ck))
            lp, hx = r("LP", l, l + ck), r("HX", 16 * l, 16 * (l + ck))
            if q == "v":
                gat("v", v, r("HD"), lp, hx)
                na = ABS if p == NPC - 1 and l + ck == L1 else 1
                for j in range(na):
                    act(r("D", ab[1] + j, ab[2], na), r("D", v[1] + j, v[2], na), F.Abs, 0.0, 2.0)
            else:
                bank = X if (l - L0) // 32 % 2 else Y
                gat("a", v, r("HD"), lp)
                mm(r(bank, 0, 16 * ck), r("Bh"), r("SR", 0, 16 * ck), True, False)
                for s in range(16):
                    mm(r(bank, s, 16 * ck, 16), r("NI"), r(hb, l, l + ck), False, False)
                mm(r(bank, 0, 16 * ck), r("ID"), v, False, True)
                act(ab, r(bank, 0, 16 * ck), F.Abs, 0.0, 2.0)
            l += ck
        pr[0] = PRI[p]
        d, y1, a2 = r(X, 0, nl), r(X, 128, 128 + nl), r(X, 0, nl)
        y0, oh, w0 = r(Y, 0, nl), r(Y, 128, 128 + nl), r(Y, 256, 256 + nl)
        k = lambda n: r(n, 0, nl)
        mms(d, [(r("Q16", 15 - s, 143 - s), r("D", 32 * L0 + s, 16 * (L0 + L1), 16))
                for s in sorted(range(16), key=lambda s: s % ABS)])
        act(x("NA"), d, F.Identity, r("TB"), -8192.0)
        tt(x("NX"), d, x("NA"), A.max)
        ts(x("NN"), x("NX"), 2, A.arith_shift_right, 15, A.bitwise_and)
        ts(x("NP"), x("NN"), r("NB"), A.add)
        mms(oh, [(r("ID"), k("OH0"))])
        tt(x("C0"), oh, x("NN"), A.mult)
        for j in range(1, 5):
            y = y1 if j % 2 else y0
            terms = [(r("ID"), x("NP"))]
            for i in range(j):
                terms.append((r("B" + "abcd"[j - 1 - i]), x("C%d" % i)))
                if i in CLA[p]:
                    terms.append((r("N" + "xyz"[j - 1 - i]), x("E%d" % i)))
            mms(y, terms)
            if j == 4 and GA[p]:
                mms(y1, terms)
            if j in CLA[p]:
                act(x("C%d" % j), y, F.Relu)
                act(x("E%d" % j), y, F.Relu, r("K16"))
            elif j < 4:
                ts(x("C%d" % j), y, 0.0, A.max, 16.0, A.min)
        if GA[p]:
            act(x("G"), y1, F.Sign, r("K15"), -1.0)
        s0, se, sx = at[p]
        wr = lambda a: r(X, 256 + a - s0, 256 + a - s0 + n4)
        mm(r(X, 256, 256 + 2 * n4), r("ID"), r("VQ", 0, 2 * n4), True, False)
        ts(x("DN"), y0, r("SC"), A.is_equal, DNS, A.mult)
        if not GA[p]:
            ts(x("G"), y0, 16.0, A.is_lt, 2.0, A.mult)
        for a in (sx, se):
            for s in range(4):
                mm(wr(a), q4("Q4", s), r("DN", L0 + s, L1, 4), False, False)
        for s in range(4):
            mm(wr(se), q4("QH", s), r("G", L0 + s, L1, 4), False, s == 3)
        one = [(r("DD"), k("ON"))] if GA[p] else []
        if TZ:
            pos, neg = ("DN8", "DP8") if last else ("DP8", "DN8")
            on = lambda n: [(r(n), k("ON"))] if GA[p] else []
            t1, t2 = r(Y, 128, 128 + nl), r(Y, 384, 384 + nl)
            mms(t1, [(r("KML" if last else "KM8"), k("ON")), (r("IF"), x("ZB"))] + on(pos) + [(r(pos), x("G"))])
            mms(t2, [(r("KM"), k("ON")), (r("IF"), x("ZM"))] + on(neg) + [(r(neg), x("G"))])
            act(x("DE"), t1, F.Copy, 0.0, -1.0 if last else 1.0)
            act(x("ZI"), t2, F.Copy, 0.0, -1.0 if last else 1.0)
        else:
            mms(oh, one + [(r("DD"), x("G"))])
            tt(x("DE"), oh, x("DZ"), A.mult)
        scan(r("ES", s0, s0 + 2 * n4), r(X, 256, 256 + 2 * n4), r("RX", s0, s0 + 2 * n4), 0.0, A.max, A.add)
        cp(r("EL", c0, c1), r("ES", se + 3, se + n4, 4))
        w = DED[p]
        if w == 1:
            ts(r("SL", 2 * c0, 2 * c1, 2), r("ES", sx + 3, sx + n4, 4), r("TR"), A.min, 4096 / DNS, A.mult)
        else:
            if DAA[p]:
                act(r("DA", 5 * c0 + 1, 5 * c1, 5), r("ES", sx + 3, sx + n4, 4), F.Copy, 0.0, 0.5 / DNS)
            else:
                ts(r("DA", 5 * c0 + 1, 5 * c1, 5), r("ES", sx + 3, sx + n4, 4), 0.5 / DNS, A.mult)
            for j in range(1, w):
                tt(r("DA", 5 * (c0 + j) + 1 + j, 5 * c1, 5), r("ES", sx + 3 + 4 * j, sx + n4, 4), r("ES", sx + 3, sx + n4 - 4 * j, 4), A.is_equal)
            scan(r("DO", 5 * c0, 5 * c1), r("DA", 5 * c0, 5 * c1), r("DB", 5 * c0, 5 * c1), 0.0, A.add, A.min)
            ts(r("SL", 2 * c0, c0 + c1), r("DO", 5 * c0 + 4, 5 * c1, 5), 8192.0, A.mult)
        tab, base, f = (r("YO"), "ZA", A.subtract) if last else (r("MZ"), "ZI", A.add)
        if TZ:
            base, f = "ZI", A.max
        for c in range(c1 - w, c0 - 1, -w):
            o0 = 2 * c if w == 1 else c0 + c
            off, de, zi, ze = r("SL", o0, o0 + w), r("DE", 16 * c, 16 * (c + w)), r(base, 16 * c, 16 * (c + w)), r("ZE", 0, 16 * w)
            op("v", lambda e, off=off, de=de, zi=zi: e.tensor_tensor(out=ap(tab).indirect(ap(off)), in0=ap(zi), in1=ap(de), op=f),
               [off, de, zi], [tab], 0.05 + 16 * w * 3.5 * CY)
            op("a", lambda e, off=off, ze=ze: e.activation(out=ap(r("NM")).indirect(ap(off)), in_=ap(ze), func=F.Silu),
               [off, ze], [r("NM")], 0.065 + 16 * w * 3.5 * CY)
        gat("a", x("DS"), r("D", 32 * L0, 32 * L1), r("EL", c0, c1))
        mm(w0, r("Be"), x("DN"), True, False)
        l = L0
        for q, ck in chunks:
            mm(r(Y, 256 + l - L0, 256 + l - L0 + ck), r("ID") if q == "a" else r("Bf"), r(hb, l, l + ck), False, l + ck == L1)
            l += ck
        act(x("AD"), w0, F.Relu, r("KB"))
        mms(a2, [(r("Bg"), k("ON")), (r("IH"), x("AD")), (r("IH"), x("DS"))])
        ts(x("hn%d" % t), a2, MAGIC, A.add, MAGIC, A.subtract)

    def send(t, h):
        c0, c1 = span(PARTS[h])
        nh, hn, arr = r("hb%d" % (t + 1), 16 * c0, 16 * c1), r("hn%d" % t, 16 * c0, 16 * c1), "ar%d_%d" % (t + 1, h)
        op("g", lambda e: e.remote_dma(ap(nh), ap(hn), T.sem[arr], T.sem.ls, pid, rid, mask),
           [hn], [nh], 1.0, sem=(arr, ne), lat=2.0)

    for t in range(STEPS):
        for h in range(len(PARTS)):
            pr[0], tag[0] = FPR[h], "f%d" % h
            front(t, h)
        for k, part in enumerate(BEFORE):
            pr[0], tag[0] = BPR[k], "b%d" % k
            before(t, part)
        for h, part in enumerate(PARTS):
            for p in part:
                pr[0], tag[0] = PRI[p], "r%d" % p
                rules(t, p)
            send(t, h)
            pr[0], tag[0] = 0.0, "e"
        if t < STEPS - 1:
            for lo, hi in zip(CUTS, CUTS[1:]):
                scan(r("ZP", 8 + lo, 8 + hi), r("NM", lo, hi), r("MZ", lo, hi), r("ZP", 7 + lo, 8 + lo) if lo else 0.0, A.add, A.min)
            act(r("ZP", 7, 8), r("ZP", W + 7, W + 8), F.Copy)
        if t == STEPS - 2:
            for lo in range(0, W, 512):
                act(r("YO", lo, lo + 512), r("MZ", lo, lo + 512), F.Abs)
    dma("s", lambda: T.yo[:], lambda: T.YO[:, 0:W], [r("YO")], [], 5.0)
    ts(r("YM", 0, W // 2), r("NM", 0, W // 2), 0.0, A.is_gt)
    act(r("YM", W // 2, W), r("NM", W // 2, W), F.Sign, r("QB"))
    dma("s", lambda: T.ym[:], lambda: T.YM[0:128:16, :], [r("YM")], [], 2.0)
    dma("s", lambda: T.yh[:], lambda: T["hb%d" % STEPS][:], [r("hb%d" % STEPS)], [], 2.0)

    emit(g, T, ops, eng, ne * STEPS * len(PARTS))


def meet(x, y):
    if x[1] >= y[2] or y[1] >= x[2]:
        return False
    return (x[1] - y[1]) % math.gcd(x[3], y[3]) == 0


def covers(x, y):
    return x[3] == 1 and x[1] <= y[1] and x[2] >= y[2]


def depend(ops):
    n = len(ops)
    dep = [dict() for _ in range(n)]
    hist, dmas = {}, {}
    for i, o in enumerate(ops):
        if o["sem"] is not None:
            if o["q"] in dmas:
                dep[i][dmas[o["q"]]] = False
            dmas[o["q"]] = i
        for wr, xs in ((False, o["rd"]), (True, o["wr"])):
            for x in xs:
                psum = x[0][:2] == "ps"
                for (j, y, w) in hist.get(x[0], []):
                    same = ops[j]["q"] == o["q"] and ops[j]["sem"] is None
                    if (wr or w) and meet(x, y):
                        wait = not same or o["q"] != "p"
                        dep[i][j] = dep[i].get(j, False) or wait
                    elif psum:
                        dep[i][j] = dep[i].get(j, False) or not same
        for wr, xs in ((False, o["rd"]), (True, o["wr"])):
            for x in xs:
                h = hist.setdefault(x[0], [])
                if wr:
                    h[:] = [z for z in h if z[0] == i or not covers(x, z[1])]
                if x[0][:2] == "ps":
                    h[:] = [z for z in h if ops[z[0]]["q"] != o["q"] or (z[2] and o["q"] != "p")]
                h.append((i, x, wr))
    return dep


def plan(ops, dep, eng):
    n = len(ops)
    succ = [[] for _ in range(n)]
    for i in range(n):
        for j in dep[i]:
            succ[j].append(i)
    tail = [0.0] * n
    for i in range(n - 1, -1, -1):
        o = ops[i]
        tail[i] = o["dur"] + max([tail[k] + (o["lat"] + HOP if dep[k][i] else 0.0) for k in succ[i]], default=o["lat"])
    left = [len(dep[i]) for i in range(n)]
    avail = [0.0] * n
    ready = {q: [] for q in eng}
    for i in range(n):
        if not left[i]:
            ready[ops[i]["q"]].append(i)
    free = {q: 0.0 for q in eng}
    order = []
    while len(order) < n:
        t0, q = min((max(free[q], min(avail[i] for i in ready[q])), q) for q in eng if ready[q])
        i = max((k for k in ready[q] if avail[k] <= t0 + 1e-9), key=lambda k: (tail[k] + ops[k]["pr"], -k))
        ready[q].remove(i)
        o = ops[i]
        free[q] = t0 + o["dur"]
        for k in succ[i]:
            avail[k] = max(avail[k], t0 + o["dur"] + o["lat"] + HOP if dep[k][i] else t0)
            left[k] -= 1
            if not left[k]:
                ready[ops[k]["q"]].append(k)
        order.append(i)
    lag = lambda j, k: ops[j]["lat"] + HOP if dep[k][j] else 0.0
    fwd = [[(j, lag(j, i)) for j in dep[i]] for i in range(n)]
    bwd = [[(k, lag(i, k)) for k in succ[i]] for i in range(n)]

    def place_all(seq, pre, head):
        end, busy = [0.0] * n, {q: [] for q in eng}
        for i in seq:
            t, d, b = max([end[j] + g0 for j, g0 in pre[i]], default=head[i]), ops[i]["dur"], busy[ops[i]["q"]]
            lo, hi = 0, len(b)
            while lo < hi:
                mid = (lo + hi) // 2
                lo, hi = (mid + 1, hi) if b[mid][1] <= t + 1e-9 else (lo, mid)
            while lo < len(b) and b[lo][0] < t + d - 1e-9:
                t = b[lo][1]
                lo += 1
            b.insert(lo, (t, t + d))
            end[i] = t + d
        return end
    best, seq, zero, lats = None, order, [0.0] * n, [o["lat"] for o in ops]
    for _ in range(ROUNDS):
        end = place_all(seq, fwd, zero)
        span = max(end[i] + lats[i] for i in range(n))
        if best is None or span < best - 1e-9:
            best, order = span, sorted(range(n), key=lambda i: (end[i] - ops[i]["dur"], i))
        LOG.append(round(span, 1))
        back = place_all(sorted(range(n), key=lambda i: (-end[i], -i)), bwd, lats)
        seq = sorted(range(n), key=lambda i: (-back[i], i))
    return order, best


def emit(g, T, ops, eng, sent):
    dep = depend(ops)
    order = plan(ops, dep, eng)[0]
    count = {q: 0 for q in eng}
    mark, know, after, place = {}, {q: {} for q in eng}, {}, {}
    final = {}
    for i in order:
        o = ops[i]
        q = o["q"]
        kn = know[q]
        for j in sorted((j for j in dep[i] if dep[i][j]), key=lambda j: -place[j]):
            s, v = mark[j]
            if kn.get(s, 0) >= v:
                continue
            eng[q].wait_ge(T.sem[s], v)
            for s2, v2 in after[j].items():
                if kn.get(s2, 0) < v2:
                    kn[s2] = v2
        ins = o["fn"](eng[q])
        remote = o["sem"] is not None and o["sem"][0][:2] == "ar"
        if o["sem"] is None:
            count[q] += 1
            mark[i] = ("q" + q, count[q])
            ins.then_inc(T.sem["q" + q], 1)
        else:
            mark[i] = o["sem"]
            if not remote:
                ins.then_inc(T.sem[o["sem"][0]], 16)
        final[mark[i][0]] = mark[i][1]
        after[i] = {} if remote else dict(kn)
        after[i][mark[i][0]] = mark[i][1]
        place[i] = len(place)
    for s, v in final.items():
        g.wait_ge(T.sem[s], v)
    g.wait_ge(T.sem.ls, sent)
